import numpy as np
import ml_dtypes


def mxq(x, axis, fmt="e4m3"):
    dtype, down = {"e4m3": (ml_dtypes.float8_e4m3fn, 7), "e5m2": (ml_dtypes.float8_e5m2, 14)}[fmt]
    v = np.moveaxis(np.asarray(x, np.float32).astype(ml_dtypes.bfloat16).astype(np.float64), axis, -1)
    blocks = v.reshape(v.shape[:-1] + (-1, 32))
    amax = np.abs(blocks).max(-1, keepdims=True)
    byte = np.maximum(np.where(amax > 0, np.frexp(amax)[1] - 1 + 127, 0) - down, 1)
    scale = np.exp2(byte - 127.0)
    codes = (blocks / scale).astype(np.float32).astype(dtype).astype(np.float64)
    return np.moveaxis((codes * scale).reshape(v.shape), -1, axis)


WIDE = False


def mx_kscale(k):
    if not WIDE:
        return np.ones(k)
    levels = np.array([10, -10, 5, -5, 0])
    if k % 512:
        return np.exp2(np.random.permutation(np.resize(levels, k // 32))).repeat(32)
    a = np.empty((k // 512, 16))
    for p in range(k // 512):
        a[p, :8] = np.random.permutation(np.resize(levels, 8))
        for g in range(8):
            far = levels[np.abs(levels - a[p, g]) >= 10]
            a[p, g + 8] = far[np.random.randint(len(far))]
    return np.exp2(a.ravel()).repeat(32)


def f64(x):
    return np.asarray(x).astype(np.float64)


def striped(idx):
    return np.tile(idx.reshape(-1, 16).T, (8, 1)).astype(np.uint16)


def unstriped(offs):
    return offs[:16].T.reshape(-1).astype(np.int64)


def relu2(v):
    return np.maximum(v, 0.0) ** 2


K, T, D, S, V, H, N = 1536, 1024, 3, 512, 256, 1024, 128


def setup_inputs():
    n = np.random.standard_normal
    s = mx_kscale(K)[:, None]
    u = mx_kscale(H)
    return {
        "xT": (n((K, T)) * s).astype(np.float32),
        "w1": (n((K, H)) / np.sqrt(K) / s * u).astype(np.float32),
        "w2": (n((H, N)) / np.sqrt(H) / u[:, None] ** 2).astype(np.float32),
        "gate": np.tile(np.random.uniform(0.2, 1.0, (D, 1, V)) / np.sqrt(D), (1, N, 1)).astype(np.float32),
        "offs": striped(np.random.permutation(T)[:S]),
        "pos1": striped(np.random.permutation(S)[:V]),
        "pos2": striped(np.random.permutation(S)[:V]),
        "pos3": striped(np.random.permutation(S)[:V]),
    }


def reference(xT, w1, w2, gate, offs, pos1, pos2, pos3):
    idx = unstriped(offs)
    xq = mxq(f64(xT)[:, idx], 0, "e4m3")
    h = relu2(mxq(f64(w1), 0, "e4m3").T @ xq)
    y = mxq(f64(w2), 0, "e4m3").T @ mxq(h, 0, "e4m3")
    return sum(f64(gate[d]) * y[:, unstriped(p)] for d, p in enumerate((pos1, pos2, pos3)))

@@ -1,0 +1,215 @@
+from contextlib import ExitStack
+
+import concourse.mybir as mybir
+
+K, T, S, H, N, D, V = 1536, 1024, 512, 1024, 128, 3, 256
+FLOPS = 2 * S * (K * H + H * N)
+
+F32 = mybir.dt.float32
+BF16 = mybir.dt.bfloat16
+U32 = mybir.dt.uint32
+U16 = mybir.dt.uint16
+U8 = mybir.dt.uint8
+FP8X4 = mybir.dt.float8_e4m3fn_x4
+ACT = mybir.ActivationFunctionType
+ALU = mybir.AluOpType
+
+P = 128
+PACK = 4
+K_PASS = P * PACK
+PASSES = K // K_PASS
+HALVES = H // K_PASS
+W = 512
+HALF = S // 2
+
+W1_SCALAR = ((112, 112, 112), (32, 32, 32))
+RELU0 = (True, False, True, True)
+RELU1 = ((True, False, True, False), (True, False, True, False))
+SQUARE = ((True, False, True, True), (True, False, True, False))
+
+
+def tile_picked_sub_mlp_relu2_sub_e_kernel(tc, xT, w1, w2, gate, offs, pos1, pos2, pos3, out):
+    nc = tc.nc
+    with ExitStack() as ctx:
+        keep = ctx.enter_context(tc.tile_pool(name="keep", bufs=1))
+        psum = ctx.enter_context(tc.psum_pool(name="psum", bufs=1))
+
+        def copy(on_scalar, dst, src):
+            if on_scalar:
+                nc.scalar.copy(dst, src)
+            else:
+                nc.vector.tensor_copy(out=dst, in_=src)
+
+        def quantize(codes, scales, grouped, cols, plane=0):
+            nc.vector.quantize_mx(
+                out=codes[:, cols].bitcast(FP8X4),
+                scales=scales[plane:P, cols],
+                in_=grouped[:, PACK * cols.start : PACK * cols.stop],
+            )
+
+        def operand(name, width):
+            return (
+                keep.tile([P, width * PACK], BF16, name=f"{name}_grouped", align_bytes=64),
+                keep.tile([P, width], U32, name=f"{name}_codes", align_bytes=64),
+                keep.tile([P, width], U8, name=f"{name}_scales", align_bytes=64),
+            )
+
+        offs_t = keep.tile([P, S // 16], U16, name="offs_t")
+        pos_t = [keep.tile([P, V // 16], U16, name=f"pos{d}_t") for d in range(D)]
+        w2_raw = keep.tile([P, HALVES, PACK, N], F32, name="w2_raw")
+        x_scales = keep.tile([P, T], U8, name="x_scales", align_bytes=64)
+        nc.gpsimd.memset(x_scales[:], 0)
+
+        def load_rows(name, source, s, first, width):
+            raw = keep.tile([P, PACK, width], F32, name=name)
+            rows = source[s * K_PASS : (s + 1) * K_PASS, first : first + width]
+            nc.sync.dma_start(out=raw[:], in_=rows.rearrange("(p j) w -> p j w", j=PACK))
+            return raw
+
+        def load_w2():
+            nc.sync.dma_start(out=w2_raw[:], in_=w2.rearrange("(g p j) m -> p g j m", p=P, j=PACK))
+
+        x_raw, w1_raw = {}, {}
+        for s in range(PASSES):
+            x_raw[s] = load_rows(f"x_raw{s}", xT, s, 0, T)
+            if s == 0:
+                nc.sync.dma_start(offs_t[:], offs)
+        for h in range(HALVES):
+            for s in range(PASSES):
+                pieces = 1
+                w1_raw[h, s] = [
+                    load_rows(f"w1_raw{h}{s}{c}", w1, s, h * W + c * (W // pieces), W // pieces) for c in range(pieces)
+                ]
+        load_w2()
+        gate_t = keep.tile([P, D, V], F32, name="gate_t")
+        nc.sync.dma_start(out=gate_t[:], in_=gate.rearrange("d m v -> m d v"))
+        for d, pos in enumerate((pos1, pos2, pos3)):
+            nc.sync.dma_start(pos_t[d][:], pos)
+
+        w2_grouped, w2_codes, w2_scales = operand("w2", HALVES * N)
+
+        def prepare_w2():
+            for g in range(HALVES):
+                nc.vector.tensor_copy(
+                    out=w2_grouped[:, g * N * PACK : (g + 1) * N * PACK].rearrange("p (c i j) -> p c j i", i=4, j=PACK),
+                    in_=w2_raw[:, g].rearrange("p j (c i) -> p c j i", i=4),
+                )
+            quantize(w2_codes, w2_scales, w2_grouped, slice(0, HALVES * N))
+
+        x_words, g_words = [], []
+
+        def gather_words(s):
+            picked = keep.tile([P, S], U32, name=f"g_words{s}", align_bytes=64)
+            nc.vector.tensor_copy(picked[:], x_words[s][:].indirect(offs_t[:]))
+            g_words.append(picked)
+
+        for s in range(PASSES):
+            words = keep.tile([P, T], U32, name=f"x_words{s}", align_bytes=64)
+            grouped = keep.tile([P, T * PACK], BF16, name=f"x_grouped{s}", align_bytes=64)
+            for c in range(T // W):
+                cols = slice(c * W, (c + 1) * W)
+                src = x_raw[s][:, :, cols].rearrange("p j (c i) -> p c j i", i=4)
+                dst = grouped[:, PACK * cols.start : PACK * cols.stop].rearrange("p (c i j) -> p c j i", i=4, j=PACK)
+                copy(c == 0, dst, src)
+            if s > 0:
+                gather_words(s - 1)
+            for c in reversed(range(T // W)):
+                quantize(words, x_scales, grouped, slice(c * W, (c + 1) * W), plane=4 * s)
+            x_words.append(words)
+        g_scales = keep.tile([P, S], U8, name="g_scales", align_bytes=64)
+
+        def gather_last():
+            gather_words(PASSES - 1)
+            nc.vector.tensor_copy(g_scales[:], x_scales[:].indirect(offs_t[:]))
+
+        def layer1(h, banks, blocks):
+            for s in range(PASSES):
+                grouped, codes, scales = operand(f"w1_{h}{s}", W)
+                pieces = w1_raw[h, s]
+                m = P // len(pieces)
+                cut = W1_SCALAR[h][s] // len(pieces)
+                for c, raw in enumerate(pieces):
+                    src = raw[:].rearrange("p j (m t) -> p m j t", t=PACK)
+                    dst = grouped[:].rearrange("p (t m j) -> p m j t", t=PACK, j=PACK)[:, c * m : (c + 1) * m]
+                    copy(True, dst[:, :cut], src[:, :cut])
+                    copy(False, dst[:, cut:], src[:, cut:])
+                if h == 0 and s == 0:
+                    gather_last()
+                step = W // 2 if h == 1 and s == PASSES - 1 else W
+                for q in range(0, W, step):
+                    quantize(codes, scales, grouped, slice(q, q + step))
+                for b, cols in enumerate(blocks):
+                    for t in range(PACK):
+                        nc.tensor.matmul_mx(
+                            out=banks[b][t][:],
+                            lhsT=codes[:, t * P : (t + 1) * P].bitcast(FP8X4),
+                            lhsT_scale=scales[:, t * P : (t + 1) * P],
+                            rhs=g_words[s][:, cols].bitcast(FP8X4),
+                            rhs_scale=g_scales[4 * s : P, cols],
+                            start=(s == 0),
+                            stop=(s == PASSES - 1),
+                        )
+
+        def relu(h, banks, blocks, on_scalar):
+            r = keep.tile([P, PACK, S], F32, name=f"r{h}")
+            for b, cols in enumerate(blocks):
+                for t in range(PACK):
+                    if on_scalar[b][t]:
+                        nc.scalar.activation(r[:, t, cols], banks[b][t][:], ACT.Relu)
+                    else:
+                        nc.vector.tensor_scalar_max(r[:, t, cols], banks[b][t][:], 0.0)
+            return r
+
+        def square(h, r):
+            grouped, codes, scales = operand(f"h{h}", S)
+            for b in range(2):
+                for q in (2 * b, 2 * b + 1):
+                    src = r[:, :, q * P : (q + 1) * P].rearrange("p t (c i) -> p c t i", i=4)
+                    dst = grouped[:, q * P * PACK : (q + 1) * P * PACK].rearrange("p (c i t) -> p c t i", i=4, t=PACK)
+                    if SQUARE[h][q]:
+                        nc.scalar.activation(dst, src, ACT.Square)
+                    else:
+                        nc.vector.tensor_tensor(dst, src, src, ALU.mult)
+                quantize(codes, scales, grouped, slice(b * HALF, (b + 1) * HALF))
+            return codes, scales
+
+        whole = [slice(0, S)]
+        halves = [slice(0, HALF), slice(HALF, S)]
+        banks0 = [[psum.tile([P, S], F32, name=f"bank0{t}", tag=f"b{t}") for t in range(PACK)]]
+        layer1(0, banks0, whole)
+        r0 = relu(0, banks0, whole, [RELU0])
+        banks1 = [
+            [psum.tile([P, HALF], F32, name=f"bank1{b}{t}", tag=f"b{4 * (1 - b) + t}") for t in range(PACK)] for b in range(2)
+        ]
+        layer1(1, banks1, halves)
+        hidden0 = square(0, r0)
+        prepare_w2()
+        r1 = relu(1, banks1, halves, RELU1)
+        hidden1 = square(1, r1)
+
+        y = keep.tile([P, S], F32, name="y")
+        y_banks = [psum.tile([P, HALF], F32, name=f"y_bank{b}", tag=f"b{4 + b}") for b in range(2)]
+        for b, cols in enumerate(halves):
+            for h, (codes, scales) in enumerate((hidden0, hidden1)):
+                nc.tensor.matmul_mx(
+                    out=y_banks[b][:],
+                    lhsT=w2_codes[:, h * N : (h + 1) * N].bitcast(FP8X4),
+                    lhsT_scale=w2_scales[:, h * N : (h + 1) * N],
+                    rhs=codes[:, cols].bitcast(FP8X4),
+                    rhs_scale=scales[:, cols],
+                    start=(h == 0),
+                    stop=(h == HALVES - 1),
+                )
+            nc.scalar.copy(y[:, cols], y_banks[b][:])
+
+        prods = [keep.tile([P, V], F32, name=f"prod{d}") for d in range(D)]
+        pair = keep.tile([P, V], F32, name="pair")
+        result = keep.tile([P, V], F32, name="result")
+        for d in range(D):
+            nc.vector.tensor_tensor(prods[d][:], y[:].indirect(pos_t[d][:]), gate_t[:, d, :], ALU.mult)
+        parts = [slice(0, V // 2), slice(V // 2, V)]
+        for part in parts:
+            nc.vector.tensor_tensor(pair[:, part], prods[0][:, part], prods[1][:, part], ALU.add)
+        for part, queue in zip(parts, (nc.sync, nc.scalar)):
+            nc.vector.tensor_tensor(result[:, part], pair[:, part], prods[2][:, part], ALU.add)
+            queue.dma_start(out=out[:, part], in_=result[:, part])

@@ -22,10 +22,17 @@ HALVES = H // K_PASS
 W = 512
 HALF = S // 2
 
-W1_SCALAR = ((112, 112, 112), (32, 32, 32))
+X_SCALAR = (112, 0)
+X_LAST_SCALAR = (112, 0)
+W1_SCALAR = ((112, 96, 48), (0, 0, 32))
+W1_PIECES = ((1, 1, 1), (1, 1, 1))
+W1_QSTEP = ((512, 512, 256), (512, 512, 256))
 RELU0 = (True, False, True, True)
-RELU1 = ((True, False, True, False), (True, False, True, False))
-SQUARE = ((True, False, True, True), (True, False, True, False))
+RELU1 = ((True, True, True, False), (True, True, True, False))
+SQUARE = ((True, True, True, True), (True, False, True, False))
+W2_SCALAR = (True, True)
+Y_BLOCKS = (256, 128, 128)
+Y_SCALAR = (True, True, False)
 
 
 def tile_picked_sub_mlp_relu2_sub_e_kernel(tc, xT, w1, w2, gate, offs, pos1, pos2, pos3, out):
@@ -40,6 +47,12 @@ def tile_picked_sub_mlp_relu2_sub_e_kernel(tc, xT, w1, w2, gate, offs, pos1, pos
             else:
                 nc.vector.tensor_copy(out=dst, in_=src)
 
+        def shared_copy(dst, src, cut):
+            if cut > 0:
+                copy(True, dst[:, :cut], src[:, :cut])
+            if cut < dst.shape[1]:
+                copy(False, dst[:, cut:], src[:, cut:])
+
         def quantize(codes, scales, grouped, cols, plane=0):
             nc.vector.quantize_mx(
                 out=codes[:, cols].bitcast(FP8X4),
@@ -47,10 +60,10 @@ def tile_picked_sub_mlp_relu2_sub_e_kernel(tc, xT, w1, w2, gate, offs, pos1, pos
                 in_=grouped[:, PACK * cols.start : PACK * cols.stop],
             )
 
-        def operand(name, width):
+        def operand(name, width, tag=None):
             return (
-                keep.tile([P, width * PACK], BF16, name=f"{name}_grouped", align_bytes=64),
-                keep.tile([P, width], U32, name=f"{name}_codes", align_bytes=64),
+                keep.tile([P, width * PACK], BF16, name=f"{name}_grouped", tag=f"{name}_grouped", align_bytes=64),
+                keep.tile([P, width], U32, name=f"{name}_codes", tag=tag or f"{name}_codes", align_bytes=64),
                 keep.tile([P, width], U8, name=f"{name}_scales", align_bytes=64),
             )
 
@@ -61,40 +74,39 @@ def tile_picked_sub_mlp_relu2_sub_e_kernel(tc, xT, w1, w2, gate, offs, pos1, pos
         nc.gpsimd.memset(x_scales[:], 0)
 
         def load_rows(name, source, s, first, width):
-            raw = keep.tile([P, PACK, width], F32, name=name)
+            raw = keep.tile([P, PACK, width], F32, name=name, tag=name, align_bytes=64)
             rows = source[s * K_PASS : (s + 1) * K_PASS, first : first + width]
             nc.sync.dma_start(out=raw[:], in_=rows.rearrange("(p j) w -> p j w", j=PACK))
             return raw
 
-        def load_w2():
-            nc.sync.dma_start(out=w2_raw[:], in_=w2.rearrange("(g p j) m -> p g j m", p=P, j=PACK))
-
         x_raw, w1_raw = {}, {}
         for s in range(PASSES):
-            x_raw[s] = load_rows(f"x_raw{s}", xT, s, 0, T)
+            raw = load_rows(f"x_raw{s}", xT, s, 0, T)
+            x_raw[s] = [raw[:, :, c * W : (c + 1) * W] for c in range(T // W)]
             if s == 0:
                 nc.sync.dma_start(offs_t[:], offs)
         for h in range(HALVES):
             for s in range(PASSES):
-                pieces = 1
+                pieces = W1_PIECES[h][s]
                 w1_raw[h, s] = [
                     load_rows(f"w1_raw{h}{s}{c}", w1, s, h * W + c * (W // pieces), W // pieces) for c in range(pieces)
                 ]
-        load_w2()
+        nc.sync.dma_start(out=w2_raw[:], in_=w2.rearrange("(g p j) m -> p g j m", p=P, j=PACK))
         gate_t = keep.tile([P, D, V], F32, name="gate_t")
         nc.sync.dma_start(out=gate_t[:], in_=gate.rearrange("d m v -> m d v"))
         for d, pos in enumerate((pos1, pos2, pos3)):
             nc.sync.dma_start(pos_t[d][:], pos)
 
-        w2_grouped, w2_codes, w2_scales = operand("w2", HALVES * N)
-
         def prepare_w2():
+            grouped, codes, scales = operand("w2", HALVES * N, tag="w1_12_codes")
             for g in range(HALVES):
-                nc.vector.tensor_copy(
-                    out=w2_grouped[:, g * N * PACK : (g + 1) * N * PACK].rearrange("p (c i j) -> p c j i", i=4, j=PACK),
-                    in_=w2_raw[:, g].rearrange("p j (c i) -> p c j i", i=4),
+                copy(
+                    W2_SCALAR[g],
+                    grouped[:, g * N * PACK : (g + 1) * N * PACK].rearrange("p (c i j) -> p c j i", i=4, j=PACK),
+                    w2_raw[:, g].rearrange("p j (c i) -> p c j i", i=4),
                 )
-            quantize(w2_codes, w2_scales, w2_grouped, slice(0, HALVES * N))
+            quantize(codes, scales, grouped, slice(0, HALVES * N))
+            return codes, scales
 
         x_words, g_words = [], []
 
@@ -108,91 +120,107 @@ def tile_picked_sub_mlp_relu2_sub_e_kernel(tc, xT, w1, w2, gate, offs, pos1, pos
             grouped = keep.tile([P, T * PACK], BF16, name=f"x_grouped{s}", align_bytes=64)
             for c in range(T // W):
                 cols = slice(c * W, (c + 1) * W)
-                src = x_raw[s][:, :, cols].rearrange("p j (c i) -> p c j i", i=4)
+                src = x_raw[s][c].rearrange("p j (c i) -> p c j i", i=4)
                 dst = grouped[:, PACK * cols.start : PACK * cols.stop].rearrange("p (c i j) -> p c j i", i=4, j=PACK)
-                copy(c == 0, dst, src)
+                shared_copy(dst, src, (X_LAST_SCALAR if s == PASSES - 1 else X_SCALAR)[c])
             if s > 0:
                 gather_words(s - 1)
             for c in reversed(range(T // W)):
                 quantize(words, x_scales, grouped, slice(c * W, (c + 1) * W), plane=4 * s)
             x_words.append(words)
         g_scales = keep.tile([P, S], U8, name="g_scales", align_bytes=64)
+        gather_words(PASSES - 1)
+        nc.vector.tensor_copy(g_scales[:], x_scales[:].indirect(offs_t[:]))
 
-        def gather_last():
-            gather_words(PASSES - 1)
-            nc.vector.tensor_copy(g_scales[:], x_scales[:].indirect(offs_t[:]))
-
-        def layer1(h, banks, blocks):
-            for s in range(PASSES):
-                grouped, codes, scales = operand(f"w1_{h}{s}", W)
-                pieces = w1_raw[h, s]
-                m = P // len(pieces)
-                cut = W1_SCALAR[h][s] // len(pieces)
-                for c, raw in enumerate(pieces):
-                    src = raw[:].rearrange("p j (m t) -> p m j t", t=PACK)
-                    dst = grouped[:].rearrange("p (t m j) -> p m j t", t=PACK, j=PACK)[:, c * m : (c + 1) * m]
-                    copy(True, dst[:, :cut], src[:, :cut])
-                    copy(False, dst[:, cut:], src[:, cut:])
-                if h == 0 and s == 0:
-                    gather_last()
-                step = W // 2 if h == 1 and s == PASSES - 1 else W
+        def layer1(h, s, banks, blocks):
+            grouped, codes, scales = operand(f"w1_{h}{s}", W)
+            pieces = w1_raw[h, s]
+            m = P // len(pieces)
+            for c, raw in enumerate(pieces):
+                src = raw[:].rearrange("p j (m t) -> p m j t", t=PACK)
+                dst = grouped[:].rearrange("p (t m j) -> p m j t", t=PACK, j=PACK)[:, c * m : (c + 1) * m]
+                shared_copy(dst, src, W1_SCALAR[h][s] // len(pieces))
+                if len(pieces) > 1:
+                    for t in range(PACK):
+                        quantize(codes, scales, grouped, slice(t * P + c * m, t * P + (c + 1) * m))
+            if len(pieces) == 1:
+                step = W1_QSTEP[h][s]
                 for q in range(0, W, step):
                     quantize(codes, scales, grouped, slice(q, q + step))
-                for b, cols in enumerate(blocks):
-                    for t in range(PACK):
-                        nc.tensor.matmul_mx(
-                            out=banks[b][t][:],
-                            lhsT=codes[:, t * P : (t + 1) * P].bitcast(FP8X4),
-                            lhsT_scale=scales[:, t * P : (t + 1) * P],
-                            rhs=g_words[s][:, cols].bitcast(FP8X4),
-                            rhs_scale=g_scales[4 * s : P, cols],
-                            start=(s == 0),
-                            stop=(s == PASSES - 1),
-                        )
-
-        def relu(h, banks, blocks, on_scalar):
-            r = keep.tile([P, PACK, S], F32, name=f"r{h}")
             for b, cols in enumerate(blocks):
                 for t in range(PACK):
-                    if on_scalar[b][t]:
-                        nc.scalar.activation(r[:, t, cols], banks[b][t][:], ACT.Relu)
-                    else:
-                        nc.vector.tensor_scalar_max(r[:, t, cols], banks[b][t][:], 0.0)
-            return r
+                    nc.tensor.matmul_mx(
+                        out=banks[b][t][:],
+                        lhsT=codes[:, t * P : (t + 1) * P].bitcast(FP8X4),
+                        lhsT_scale=scales[:, t * P : (t + 1) * P],
+                        rhs=g_words[s][:, cols].bitcast(FP8X4),
+                        rhs_scale=g_scales[4 * s : P, cols],
+                        start=(s == 0),
+                        stop=(s == PASSES - 1),
+                    )
 
-        def square(h, r):
-            grouped, codes, scales = operand(f"h{h}", S)
-            for b in range(2):
-                for q in (2 * b, 2 * b + 1):
-                    src = r[:, :, q * P : (q + 1) * P].rearrange("p t (c i) -> p c t i", i=4)
-                    dst = grouped[:, q * P * PACK : (q + 1) * P * PACK].rearrange("p (c i t) -> p c t i", i=4, t=PACK)
-                    if SQUARE[h][q]:
-                        nc.scalar.activation(dst, src, ACT.Square)
-                    else:
-                        nc.vector.tensor_tensor(dst, src, src, ALU.mult)
-                quantize(codes, scales, grouped, slice(b * HALF, (b + 1) * HALF))
-            return codes, scales
+        def relu(r, banks, cols, on_scalar):
+            for t in range(PACK):
+                if on_scalar[t]:
+                    nc.scalar.activation(r[:, t, cols], banks[t][:], ACT.Relu)
+                else:
+                    nc.vector.tensor_scalar_max(r[:, t, cols], banks[t][:], 0.0)
+
+        def square(h, r, grouped, q, at):
+            src = r[:, :, q * P : (q + 1) * P].rearrange("p t (c i) -> p c t i", i=4)
+            dst = grouped[:, at * P * PACK : (at + 1) * P * PACK].rearrange("p (c i t) -> p c t i", i=4, t=PACK)
+            if SQUARE[h][q]:
+                nc.scalar.activation(dst, src, ACT.Square)
+            else:
+                nc.vector.tensor_tensor(dst, src, src, ALU.mult)
 
         whole = [slice(0, S)]
         halves = [slice(0, HALF), slice(HALF, S)]
         banks0 = [[psum.tile([P, S], F32, name=f"bank0{t}", tag=f"b{t}") for t in range(PACK)]]
-        layer1(0, banks0, whole)
-        r0 = relu(0, banks0, whole, [RELU0])
+        for s in range(PASSES):
+            layer1(0, s, banks0, whole)
+        r0 = keep.tile([P, PACK, S], F32, name="r0")
+        relu(r0, banks0[0], whole[0], RELU0)
         banks1 = [
             [psum.tile([P, HALF], F32, name=f"bank1{b}{t}", tag=f"b{4 * (1 - b) + t}") for t in range(PACK)] for b in range(2)
         ]
-        layer1(1, banks1, halves)
-        hidden0 = square(0, r0)
-        prepare_w2()
-        r1 = relu(1, banks1, halves, RELU1)
-        hidden1 = square(1, r1)
+        grouped0 = [
+            keep.tile([P, P * PACK * n], BF16, name=f"h0_grouped{b}", tag=tag, align_bytes=64)
+            for b, (n, tag) in enumerate(((4, "h0_grouped0"), (0, "w1_raw120")))
+            if n
+        ]
+        for q in range(4):
+            square(0, r0, grouped0[0], q, q)
+        for s in range(PASSES):
+            layer1(1, s, banks1, halves)
+        for q in range(4, 4):
+            square(0, r0, grouped0[-1], q, q - 4)
+        codes0 = keep.tile([P, S], U32, name="h0_codes", tag="w1_12_grouped", align_bytes=64)
+        scales0 = keep.tile([P, S], U8, name="h0_scales", align_bytes=64)
+        for first, width, grouped in ((0, 512, grouped0[0][:]),):
+            nc.vector.quantize_mx(
+                out=codes0[:, first : first + width].bitcast(FP8X4),
+                scales=scales0[:, first : first + width],
+                in_=grouped,
+            )
+        w2_codes, w2_scales = prepare_w2()
+        r1 = keep.tile([P, PACK, S], F32, name="r1")
+        grouped1, codes1, scales1 = operand("h1", S)
+        for b in range(2):
+            relu(r1, banks1[b], halves[b], RELU1[b])
+        for q in range(4):
+            square(1, r1, grouped1, q, q)
 
         y = keep.tile([P, S], F32, name="y")
-        y_banks = [psum.tile([P, HALF], F32, name=f"y_bank{b}", tag=f"b{4 + b}") for b in range(2)]
-        for b, cols in enumerate(halves):
-            for h, (codes, scales) in enumerate((hidden0, hidden1)):
+        first = 0
+        for b, width in enumerate(Y_BLOCKS):
+            cols = slice(first, first + width)
+            first = first + width
+            y_bank = psum.tile([P, width], F32, name=f"y_bank{b}", tag=f"b{4 + b}")
+            quantize(codes1, scales1, grouped1, cols)
+            for h, (codes, scales) in enumerate(((codes0, scales0), (codes1, scales1))):
                 nc.tensor.matmul_mx(
-                    out=y_banks[b][:],
+                    out=y_bank[:],
                     lhsT=w2_codes[:, h * N : (h + 1) * N].bitcast(FP8X4),
                     lhsT_scale=w2_scales[:, h * N : (h + 1) * N],
                     rhs=codes[:, cols].bitcast(FP8X4),
@@ -200,7 +228,7 @@ def tile_picked_sub_mlp_relu2_sub_e_kernel(tc, xT, w1, w2, gate, offs, pos1, pos
                     start=(h == 0),
                     stop=(h == HALVES - 1),
                 )
-            nc.scalar.copy(y[:, cols], y_banks[b][:])
+            copy(Y_SCALAR[b], y[:, cols], y_bank[:])
 
         prods = [keep.tile([P, V], F32, name=f"prod{d}") for d in range(D)]
         pair = keep.tile([P, V], F32, name="pair")

@@ -22,12 +22,11 @@ HALVES = H // K_PASS
 W = 512
 HALF = S // 2
 
-X_SCALAR = (112, 0)
-X_LAST_SCALAR = (112, 0)
-W1_SCALAR = ((112, 96, 48), (0, 0, 32))
-W1_PIECES = ((1, 1, 1), (1, 1, 1))
+X_SCALAR = ((0, 104), (0, 104), (0, 112))
+X_PIECES = (1, 1, 1)
+W1_SCALAR = ((128, 112, 64), (64, 0, 16))
 W1_QSTEP = ((512, 512, 256), (512, 512, 256))
-RELU0 = (True, False, True, True)
+RELU0 = (True, True, True, False)
 RELU1 = ((True, True, True, False), (True, True, True, False))
 SQUARE = ((True, True, True, True), (True, False, True, False))
 W2_SCALAR = (True, True)
@@ -40,6 +39,9 @@ def tile_picked_sub_mlp_relu2_sub_e_kernel(tc, xT, w1, w2, gate, offs, pos1, pos
     with ExitStack() as ctx:
         keep = ctx.enter_context(tc.tile_pool(name="keep", bufs=1))
         psum = ctx.enter_context(tc.psum_pool(name="psum", bufs=1))
+
+        def tile(shape, dtype, name, tag=None):
+            return keep.tile(shape, dtype, name=name, tag=tag or name, align_bytes=64)
 
         def copy(on_scalar, dst, src):
             if on_scalar:
@@ -60,93 +62,67 @@ def tile_picked_sub_mlp_relu2_sub_e_kernel(tc, xT, w1, w2, gate, offs, pos1, pos
                 in_=grouped[:, PACK * cols.start : PACK * cols.stop],
             )
 
-        def operand(name, width, tag=None):
-            return (
-                keep.tile([P, width * PACK], BF16, name=f"{name}_grouped", tag=f"{name}_grouped", align_bytes=64),
-                keep.tile([P, width], U32, name=f"{name}_codes", tag=tag or f"{name}_codes", align_bytes=64),
-                keep.tile([P, width], U8, name=f"{name}_scales", align_bytes=64),
-            )
-
         offs_t = keep.tile([P, S // 16], U16, name="offs_t")
         pos_t = [keep.tile([P, V // 16], U16, name=f"pos{d}_t") for d in range(D)]
-        w2_raw = keep.tile([P, HALVES, PACK, N], F32, name="w2_raw")
-        x_scales = keep.tile([P, T], U8, name="x_scales", align_bytes=64)
+        x_scales = tile([P, T], U8, "x_scales")
         nc.gpsimd.memset(x_scales[:], 0)
 
         def load_rows(name, source, s, first, width):
-            raw = keep.tile([P, PACK, width], F32, name=name, tag=name, align_bytes=64)
+            raw = tile([P, PACK, width], F32, name)
             rows = source[s * K_PASS : (s + 1) * K_PASS, first : first + width]
             nc.sync.dma_start(out=raw[:], in_=rows.rearrange("(p j) w -> p j w", j=PACK))
             return raw
 
         x_raw, w1_raw = {}, {}
         for s in range(PASSES):
-            raw = load_rows(f"x_raw{s}", xT, s, 0, T)
-            x_raw[s] = [raw[:, :, c * W : (c + 1) * W] for c in range(T // W)]
+            if X_PIECES[s] == 1:
+                raw = load_rows(f"x_raw{s}", xT, s, 0, T)
+                x_raw[s] = [raw[:, :, c * W : (c + 1) * W] for c in range(T // W)]
+            else:
+                x_raw[s] = [load_rows(f"x_raw{s}{c}", xT, s, c * W, W)[:] for c in range(T // W)]
             if s == 0:
                 nc.sync.dma_start(offs_t[:], offs)
         for h in range(HALVES):
             for s in range(PASSES):
-                pieces = W1_PIECES[h][s]
-                w1_raw[h, s] = [
-                    load_rows(f"w1_raw{h}{s}{c}", w1, s, h * W + c * (W // pieces), W // pieces) for c in range(pieces)
-                ]
+                w1_raw[h, s] = load_rows(f"w1_raw{h}{s}", w1, s, h * W, W)
+        w2_raw = tile([P, HALVES, PACK, N], F32, "w2_raw")
         nc.sync.dma_start(out=w2_raw[:], in_=w2.rearrange("(g p j) m -> p g j m", p=P, j=PACK))
-        gate_t = keep.tile([P, D, V], F32, name="gate_t")
+        gate_t = tile([P, D, V], F32, "gate_t")
         nc.sync.dma_start(out=gate_t[:], in_=gate.rearrange("d m v -> m d v"))
         for d, pos in enumerate((pos1, pos2, pos3)):
             nc.sync.dma_start(pos_t[d][:], pos)
 
-        def prepare_w2():
-            grouped, codes, scales = operand("w2", HALVES * N, tag="w1_12_codes")
-            for g in range(HALVES):
-                copy(
-                    W2_SCALAR[g],
-                    grouped[:, g * N * PACK : (g + 1) * N * PACK].rearrange("p (c i j) -> p c j i", i=4, j=PACK),
-                    w2_raw[:, g].rearrange("p j (c i) -> p c j i", i=4),
-                )
-            quantize(codes, scales, grouped, slice(0, HALVES * N))
-            return codes, scales
-
-        x_words, g_words = [], []
-
-        def gather_words(s):
-            picked = keep.tile([P, S], U32, name=f"g_words{s}", align_bytes=64)
-            nc.vector.tensor_copy(picked[:], x_words[s][:].indirect(offs_t[:]))
-            g_words.append(picked)
-
+        g_words = []
         for s in range(PASSES):
-            words = keep.tile([P, T], U32, name=f"x_words{s}", align_bytes=64)
-            grouped = keep.tile([P, T * PACK], BF16, name=f"x_grouped{s}", align_bytes=64)
+            words = tile([P, T], U32, f"x_words{s}")
+            grouped = tile([P, T * PACK], BF16, f"x_grouped{s}")
             for c in range(T // W):
-                cols = slice(c * W, (c + 1) * W)
                 src = x_raw[s][c].rearrange("p j (c i) -> p c j i", i=4)
-                dst = grouped[:, PACK * cols.start : PACK * cols.stop].rearrange("p (c i j) -> p c j i", i=4, j=PACK)
-                shared_copy(dst, src, (X_LAST_SCALAR if s == PASSES - 1 else X_SCALAR)[c])
-            if s > 0:
-                gather_words(s - 1)
-            for c in reversed(range(T // W)):
+                dst = grouped[:, PACK * W * c : PACK * W * (c + 1)].rearrange("p (c i j) -> p c j i", i=4, j=PACK)
+                shared_copy(dst, src, X_SCALAR[s][c])
+            for c in range(T // W):
                 quantize(words, x_scales, grouped, slice(c * W, (c + 1) * W), plane=4 * s)
-            x_words.append(words)
-        g_scales = keep.tile([P, S], U8, name="g_scales", align_bytes=64)
-        gather_words(PASSES - 1)
+            if s < PASSES - 1:
+                picked = tile([P, S], U32, f"g_words{s}")
+                nc.vector.tensor_copy(picked[:], words[:].indirect(offs_t[:]))
+                g_words.append(picked)
+        g_scales = tile([P, S], U8, "g_scales")
         nc.vector.tensor_copy(g_scales[:], x_scales[:].indirect(offs_t[:]))
 
-        def layer1(h, s, banks, blocks):
-            grouped, codes, scales = operand(f"w1_{h}{s}", W)
-            pieces = w1_raw[h, s]
-            m = P // len(pieces)
-            for c, raw in enumerate(pieces):
-                src = raw[:].rearrange("p j (m t) -> p m j t", t=PACK)
-                dst = grouped[:].rearrange("p (t m j) -> p m j t", t=PACK, j=PACK)[:, c * m : (c + 1) * m]
-                shared_copy(dst, src, W1_SCALAR[h][s] // len(pieces))
-                if len(pieces) > 1:
-                    for t in range(PACK):
-                        quantize(codes, scales, grouped, slice(t * P + c * m, t * P + (c + 1) * m))
-            if len(pieces) == 1:
-                step = W1_QSTEP[h][s]
-                for q in range(0, W, step):
-                    quantize(codes, scales, grouped, slice(q, q + step))
+        def prepare_w1(h, s):
+            grouped = tile([P, W * PACK], BF16, f"w1_{h}{s}_grouped")
+            codes = tile([P, W], U32, f"w1_{h}{s}_codes")
+            scales = tile([P, W], U8, f"w1_{h}{s}_scales")
+            src = w1_raw[h, s][:].rearrange("p j (m t) -> p m j t", t=PACK)
+            dst = grouped[:].rearrange("p (t m j) -> p m j t", t=PACK, j=PACK)
+            shared_copy(dst, src, W1_SCALAR[h][s])
+            step = W1_QSTEP[h][s]
+            for q in range(0, W, step):
+                quantize(codes, scales, grouped, slice(q, q + step))
+            return codes, scales
+
+        def multiply(s, weights, banks, blocks):
+            codes, scales = weights
             for b, cols in enumerate(blocks):
                 for t in range(PACK):
                     nc.tensor.matmul_mx(
@@ -166,9 +142,9 @@ def tile_picked_sub_mlp_relu2_sub_e_kernel(tc, xT, w1, w2, gate, offs, pos1, pos
                 else:
                     nc.vector.tensor_scalar_max(r[:, t, cols], banks[t][:], 0.0)
 
-        def square(h, r, grouped, q, at):
+        def square(h, r, grouped, q):
             src = r[:, :, q * P : (q + 1) * P].rearrange("p t (c i) -> p c t i", i=4)
-            dst = grouped[:, at * P * PACK : (at + 1) * P * PACK].rearrange("p (c i t) -> p c t i", i=4, t=PACK)
+            dst = grouped[:, q * P * PACK : (q + 1) * P * PACK].rearrange("p (c i t) -> p c t i", i=4, t=PACK)
             if SQUARE[h][q]:
                 nc.scalar.activation(dst, src, ACT.Square)
             else:
@@ -178,40 +154,49 @@ def tile_picked_sub_mlp_relu2_sub_e_kernel(tc, xT, w1, w2, gate, offs, pos1, pos
         halves = [slice(0, HALF), slice(HALF, S)]
         banks0 = [[psum.tile([P, S], F32, name=f"bank0{t}", tag=f"b{t}") for t in range(PACK)]]
         for s in range(PASSES):
-            layer1(0, s, banks0, whole)
-        r0 = keep.tile([P, PACK, S], F32, name="r0")
+            multiply(s, prepare_w1(0, s), banks0, whole)
+            if s == 0:
+                picked = tile([P, S], U32, "g_words2", tag="w1_00_grouped")
+                nc.vector.tensor_copy(picked[:], words[:].indirect(offs_t[:]))
+                g_words.append(picked)
+        weights = [prepare_w1(1, 0)]
+        r0 = tile([P, PACK, S], F32, "r0", tag="w1_raw10")
         relu(r0, banks0[0], whole[0], RELU0)
+        grouped0 = tile([P, S * PACK], BF16, "h0_grouped")
+        for q in range(4):
+            square(0, r0, grouped0, q)
         banks1 = [
             [psum.tile([P, HALF], F32, name=f"bank1{b}{t}", tag=f"b{4 * (1 - b) + t}") for t in range(PACK)] for b in range(2)
         ]
-        grouped0 = [
-            keep.tile([P, P * PACK * n], BF16, name=f"h0_grouped{b}", tag=tag, align_bytes=64)
-            for b, (n, tag) in enumerate(((4, "h0_grouped0"), (0, "w1_raw120")))
-            if n
-        ]
-        for q in range(4):
-            square(0, r0, grouped0[0], q, q)
         for s in range(PASSES):
-            layer1(1, s, banks1, halves)
-        for q in range(4, 4):
-            square(0, r0, grouped0[-1], q, q - 4)
-        codes0 = keep.tile([P, S], U32, name="h0_codes", tag="w1_12_grouped", align_bytes=64)
-        scales0 = keep.tile([P, S], U8, name="h0_scales", align_bytes=64)
-        for first, width, grouped in ((0, 512, grouped0[0][:]),):
-            nc.vector.quantize_mx(
-                out=codes0[:, first : first + width].bitcast(FP8X4),
-                scales=scales0[:, first : first + width],
-                in_=grouped,
+            if s >= len(weights):
+                weights.append(prepare_w1(1, s))
+            multiply(s, weights[s], banks1, halves)
+        codes0 = tile([P, S], U32, "h0_codes", tag="w1_12_grouped")
+        scales0 = tile([P, S], U8, "h0_scales")
+        quantize(codes0, scales0, grouped0, whole[0])
+
+        w2_grouped = tile([P, HALVES * N * PACK], BF16, "w2_grouped")
+        w2_codes = tile([P, HALVES * N], U32, "w2_codes", tag="w1_12_codes")
+        w2_scales = tile([P, HALVES * N], U8, "w2_scales")
+        for g in range(HALVES):
+            copy(
+                W2_SCALAR[g],
+                w2_grouped[:, g * N * PACK : (g + 1) * N * PACK].rearrange("p (c i j) -> p c j i", i=4, j=PACK),
+                w2_raw[:, g].rearrange("p j (c i) -> p c j i", i=4),
             )
-        w2_codes, w2_scales = prepare_w2()
-        r1 = keep.tile([P, PACK, S], F32, name="r1")
-        grouped1, codes1, scales1 = operand("h1", S)
+        quantize(w2_codes, w2_scales, w2_grouped, slice(0, HALVES * N))
+
+        r1 = tile([P, PACK, S], F32, "r1")
+        grouped1 = tile([P, S * PACK], BF16, "h1_grouped")
+        codes1 = tile([P, S], U32, "h1_codes")
+        scales1 = tile([P, S], U8, "h1_scales")
         for b in range(2):
             relu(r1, banks1[b], halves[b], RELU1[b])
         for q in range(4):
-            square(1, r1, grouped1, q, q)
+            square(1, r1, grouped1, q)
 
-        y = keep.tile([P, S], F32, name="y")
+        y = tile([P, S], F32, "y")
         first = 0
         for b, width in enumerate(Y_BLOCKS):
             cols = slice(first, first + width)
@@ -230,9 +215,9 @@ def tile_picked_sub_mlp_relu2_sub_e_kernel(tc, xT, w1, w2, gate, offs, pos1, pos
                 )
             copy(Y_SCALAR[b], y[:, cols], y_bank[:])
 
-        prods = [keep.tile([P, V], F32, name=f"prod{d}") for d in range(D)]
-        pair = keep.tile([P, V], F32, name="pair")
-        result = keep.tile([P, V], F32, name="result")
+        prods = [tile([P, V], F32, f"prod{d}") for d in range(D)]
+        pair = tile([P, V], F32, "pair")
+        result = tile([P, V], F32, "result")
         for d in range(D):
             nc.vector.tensor_tensor(prods[d][:], y[:].indirect(pos_t[d][:]), gate_t[:, d, :], ALU.mult)
         parts = [slice(0, V // 2), slice(V // 2, V)]

@@ -22,16 +22,16 @@ HALVES = H // K_PASS
 W = 512
 HALF = S // 2
 
-X_SCALAR = ((0, 104), (0, 104), (0, 112))
+X_SCALAR = ((0, 120), (0, 120), (0, 112))
 X_PIECES = (1, 1, 1)
-W1_SCALAR = ((128, 112, 64), (64, 0, 16))
+W1_SCALAR = ((128, 112, 72), (0, 0, 0))
 W1_QSTEP = ((512, 512, 256), (512, 512, 256))
-RELU0 = (True, True, True, False)
+RELU0 = (True, True, True, True)
 RELU1 = ((True, True, True, False), (True, True, True, False))
 SQUARE = ((True, True, True, True), (True, False, True, False))
 W2_SCALAR = (True, True)
 Y_BLOCKS = (256, 128, 128)
-Y_SCALAR = (True, True, False)
+Y_SCALAR = (True, False, False)
 
 
 def tile_picked_sub_mlp_relu2_sub_e_kernel(tc, xT, w1, w2, gate, offs, pos1, pos2, pos3, out):
@@ -160,11 +160,15 @@ def tile_picked_sub_mlp_relu2_sub_e_kernel(tc, xT, w1, w2, gate, offs, pos1, pos
                 nc.vector.tensor_copy(picked[:], words[:].indirect(offs_t[:]))
                 g_words.append(picked)
         weights = [prepare_w1(1, 0)]
-        r0 = tile([P, PACK, S], F32, "r0", tag="w1_raw10")
+        r0 = tile([P, PACK, S], F32, "r0")
         relu(r0, banks0[0], whole[0], RELU0)
         grouped0 = tile([P, S * PACK], BF16, "h0_grouped")
-        for q in range(4):
-            square(0, r0, grouped0, q)
+        for cols in halves:
+            nc.scalar.activation(
+                grouped0[:, PACK * cols.start : PACK * cols.stop].rearrange("p (c i t) -> p c t i", i=4, t=PACK),
+                r0[:, :, cols].rearrange("p t (c i) -> p c t i", i=4),
+                ACT.Square,
+            )
         banks1 = [
             [psum.tile([P, HALF], F32, name=f"bank1{b}{t}", tag=f"b{4 * (1 - b) + t}") for t in range(PACK)] for b in range(2)
         ]
@@ -179,12 +183,10 @@ def tile_picked_sub_mlp_relu2_sub_e_kernel(tc, xT, w1, w2, gate, offs, pos1, pos
         w2_grouped = tile([P, HALVES * N * PACK], BF16, "w2_grouped")
         w2_codes = tile([P, HALVES * N], U32, "w2_codes", tag="w1_12_codes")
         w2_scales = tile([P, HALVES * N], U8, "w2_scales")
-        for g in range(HALVES):
-            copy(
-                W2_SCALAR[g],
-                w2_grouped[:, g * N * PACK : (g + 1) * N * PACK].rearrange("p (c i j) -> p c j i", i=4, j=PACK),
-                w2_raw[:, g].rearrange("p j (c i) -> p c j i", i=4),
-            )
+        nc.scalar.copy(
+            w2_grouped[:].rearrange("p (g c i j) -> p g c j i", g=HALVES, i=4, j=PACK),
+            w2_raw[:].rearrange("p g j (c i) -> p g c j i", i=4),
+        )
         quantize(w2_codes, w2_scales, w2_grouped, slice(0, HALVES * N))
 
         r1 = tile([P, PACK, S], F32, "r1")

@@ -18,20 +18,14 @@ P = 128
 PACK = 4
 K_PASS = P * PACK
 PASSES = K // K_PASS
-HALVES = H // K_PASS
+GROUPS = H // K_PASS
 W = 512
+RUN = 4
 HALF = S // 2
 
-X_SCALAR = ((0, 120), (0, 120), (0, 112))
-X_PIECES = (1, 1, 1)
-W1_SCALAR = ((128, 112, 72), (0, 0, 0))
-W1_QSTEP = ((512, 512, 256), (512, 512, 256))
-RELU0 = (True, True, True, True)
-RELU1 = ((True, True, True, False), (True, True, True, False))
-SQUARE = ((True, True, True, True), (True, False, True, False))
-W2_SCALAR = (True, True)
-Y_BLOCKS = (256, 128, 128)
-Y_SCALAR = (True, False, False)
+X_RUNS_ON_SCALAR = 112
+W1_ROWS_ON_VECTOR = ((32, 32, P), (2 * P, 2 * P, 2 * P))
+Y_BLOCKS = (slice(0, 256), slice(256, 384), slice(384, 512))
 
 
 def tile_picked_sub_mlp_relu2_sub_e_kernel(tc, xT, w1, w2, gate, offs, pos1, pos2, pos3, out):
@@ -40,8 +34,8 @@ def tile_picked_sub_mlp_relu2_sub_e_kernel(tc, xT, w1, w2, gate, offs, pos1, pos
         keep = ctx.enter_context(tc.tile_pool(name="keep", bufs=1))
         psum = ctx.enter_context(tc.psum_pool(name="psum", bufs=1))
 
-        def tile(shape, dtype, name, tag=None):
-            return keep.tile(shape, dtype, name=name, tag=tag or name, align_bytes=64)
+        def tile(shape, dtype, name, reuses=None):
+            return keep.tile(shape, dtype, name=name, tag=reuses or name, align_bytes=64)
 
         def copy(on_scalar, dst, src):
             if on_scalar:
@@ -49,17 +43,17 @@ def tile_picked_sub_mlp_relu2_sub_e_kernel(tc, xT, w1, w2, gate, offs, pos1, pos
             else:
                 nc.vector.tensor_copy(out=dst, in_=src)
 
-        def shared_copy(dst, src, cut):
-            if cut > 0:
-                copy(True, dst[:, :cut], src[:, :cut])
-            if cut < dst.shape[1]:
-                copy(False, dst[:, cut:], src[:, cut:])
-
-        def quantize(codes, scales, grouped, cols, plane=0):
+        def quantize(words, scales, grouped, cols, scale_row=0):
             nc.vector.quantize_mx(
-                out=codes[:, cols].bitcast(FP8X4),
-                scales=scales[plane:P, cols],
+                out=words[:, cols].bitcast(FP8X4),
+                scales=scales[scale_row:P, cols],
                 in_=grouped[:, PACK * cols.start : PACK * cols.stop],
+            )
+
+        def interleaved(grouped, planes):
+            return (
+                grouped.rearrange("p (c i j) -> p c j i", i=RUN, j=PACK),
+                planes.rearrange("p j (c i) -> p c j i", i=RUN),
             )
 
         offs_t = keep.tile([P, S // 16], U16, name="offs_t")
@@ -73,158 +67,148 @@ def tile_picked_sub_mlp_relu2_sub_e_kernel(tc, xT, w1, w2, gate, offs, pos1, pos
             nc.sync.dma_start(out=raw[:], in_=rows.rearrange("(p j) w -> p j w", j=PACK))
             return raw
 
-        x_raw, w1_raw = {}, {}
-        for s in range(PASSES):
-            if X_PIECES[s] == 1:
-                raw = load_rows(f"x_raw{s}", xT, s, 0, T)
-                x_raw[s] = [raw[:, :, c * W : (c + 1) * W] for c in range(T // W)]
-            else:
-                x_raw[s] = [load_rows(f"x_raw{s}{c}", xT, s, c * W, W)[:] for c in range(T // W)]
-            if s == 0:
-                nc.sync.dma_start(offs_t[:], offs)
-        for h in range(HALVES):
-            for s in range(PASSES):
-                w1_raw[h, s] = load_rows(f"w1_raw{h}{s}", w1, s, h * W, W)
-        w2_raw = tile([P, HALVES, PACK, N], F32, "w2_raw")
+        x_raw = [load_rows("x_raw0", xT, 0, 0, T)]
+        nc.sync.dma_start(offs_t[:], offs)
+        x_raw.extend(load_rows(f"x_raw{s}", xT, s, 0, T) for s in range(1, PASSES))
+        w1_raw = [[load_rows(f"w1_raw{g}{s}", w1, s, g * W, W) for s in range(PASSES)] for g in range(GROUPS)]
+        w2_raw = tile([P, GROUPS, PACK, N], F32, "w2_raw")
         nc.sync.dma_start(out=w2_raw[:], in_=w2.rearrange("(g p j) m -> p g j m", p=P, j=PACK))
         gate_t = tile([P, D, V], F32, "gate_t")
         nc.sync.dma_start(out=gate_t[:], in_=gate.rearrange("d m v -> m d v"))
         for d, pos in enumerate((pos1, pos2, pos3)):
             nc.sync.dma_start(pos_t[d][:], pos)
 
-        g_words = []
+        x_words, picked_words = [], []
+
+        def gather_words(s, reuses=None):
+            picked = tile([P, S], U32, f"picked_words{s}", reuses)
+            nc.vector.tensor_copy(picked[:], x_words[s][:].indirect(offs_t[:]))
+            picked_words.append(picked)
+
+        chunks = [slice(0, W), slice(W, T)]
         for s in range(PASSES):
             words = tile([P, T], U32, f"x_words{s}")
             grouped = tile([P, T * PACK], BF16, f"x_grouped{s}")
-            for c in range(T // W):
-                src = x_raw[s][c].rearrange("p j (c i) -> p c j i", i=4)
-                dst = grouped[:, PACK * W * c : PACK * W * (c + 1)].rearrange("p (c i j) -> p c j i", i=4, j=PACK)
-                shared_copy(dst, src, X_SCALAR[s][c])
-            for c in range(T // W):
-                quantize(words, x_scales, grouped, slice(c * W, (c + 1) * W), plane=4 * s)
+            copy(False, *interleaved(grouped[:, : W * PACK], x_raw[s][:, :, chunks[0]]))
+            dst, src = interleaved(grouped[:, W * PACK :], x_raw[s][:, :, chunks[1]])
+            copy(True, dst[:, :X_RUNS_ON_SCALAR], src[:, :X_RUNS_ON_SCALAR])
+            copy(False, dst[:, X_RUNS_ON_SCALAR:], src[:, X_RUNS_ON_SCALAR:])
+            for cols in chunks:
+                quantize(words, x_scales, grouped, cols, scale_row=4 * s)
+            x_words.append(words)
             if s < PASSES - 1:
-                picked = tile([P, S], U32, f"g_words{s}")
-                nc.vector.tensor_copy(picked[:], words[:].indirect(offs_t[:]))
-                g_words.append(picked)
-        g_scales = tile([P, S], U8, "g_scales")
-        nc.vector.tensor_copy(g_scales[:], x_scales[:].indirect(offs_t[:]))
+                gather_words(s)
+        picked_scales = tile([P, S], U8, "picked_scales")
+        nc.vector.tensor_copy(picked_scales[:], x_scales[:].indirect(offs_t[:]))
 
-        def prepare_w1(h, s):
-            grouped = tile([P, W * PACK], BF16, f"w1_{h}{s}_grouped")
-            codes = tile([P, W], U32, f"w1_{h}{s}_codes")
-            scales = tile([P, W], U8, f"w1_{h}{s}_scales")
-            src = w1_raw[h, s][:].rearrange("p j (m t) -> p m j t", t=PACK)
-            dst = grouped[:].rearrange("p (t m j) -> p m j t", t=PACK, j=PACK)
-            shared_copy(dst, src, W1_SCALAR[h][s])
-            step = W1_QSTEP[h][s]
-            for q in range(0, W, step):
-                quantize(codes, scales, grouped, slice(q, q + step))
-            return codes, scales
+        def prepare_w1(g, s):
+            grouped = tile([P, W * PACK], BF16, f"w1_grouped{g}{s}")
+            words = tile([P, W], U32, f"w1_words{g}{s}")
+            scales = tile([P, W], U8, f"w1_scales{g}{s}")
+            src = w1_raw[g][s][:].rearrange("p j (m u e) -> p u m j e", u=2, e=2)
+            dst = grouped[:].rearrange("p (u e m j) -> p u m j e", u=2, e=2, j=PACK)
+            for u in range(2):
+                cut = min(max(W1_ROWS_ON_VECTOR[g][s] - u * P, 0), P)
+                if cut > 0:
+                    copy(False, dst[:, u, :cut], src[:, u, :cut])
+                if cut < P:
+                    copy(True, dst[:, u, cut:], src[:, u, cut:])
+            for u in range(2):
+                quantize(words, scales, grouped, slice(2 * u * P, 2 * (u + 1) * P))
+            return words, scales
 
-        def multiply(s, weights, banks, blocks):
-            codes, scales = weights
-            for b, cols in enumerate(blocks):
+        def layer1_pass(s, weights, banks, blocks):
+            words, scales = weights
+            for block_banks, cols in zip(banks, blocks):
                 for t in range(PACK):
                     nc.tensor.matmul_mx(
-                        out=banks[b][t][:],
-                        lhsT=codes[:, t * P : (t + 1) * P].bitcast(FP8X4),
+                        out=block_banks[t][:],
+                        lhsT=words[:, t * P : (t + 1) * P].bitcast(FP8X4),
                         lhsT_scale=scales[:, t * P : (t + 1) * P],
-                        rhs=g_words[s][:, cols].bitcast(FP8X4),
-                        rhs_scale=g_scales[4 * s : P, cols],
+                        rhs=picked_words[s][:, cols].bitcast(FP8X4),
+                        rhs_scale=picked_scales[4 * s : P, cols],
                         start=(s == 0),
                         stop=(s == PASSES - 1),
                     )
 
-        def relu(r, banks, cols, on_scalar):
-            for t in range(PACK):
-                if on_scalar[t]:
-                    nc.scalar.activation(r[:, t, cols], banks[t][:], ACT.Relu)
-                else:
-                    nc.vector.tensor_scalar_max(r[:, t, cols], banks[t][:], 0.0)
+        whole = slice(0, S)
+        halves = [slice(0, HALF), slice(HALF, S)]
 
-        def square(h, r, grouped, q):
-            src = r[:, :, q * P : (q + 1) * P].rearrange("p t (c i) -> p c t i", i=4)
-            dst = grouped[:, q * P * PACK : (q + 1) * P * PACK].rearrange("p (c i t) -> p c t i", i=4, t=PACK)
-            if SQUARE[h][q]:
+        banks0 = [psum.tile([P, S], F32, name=f"bank0{t}", tag=f"b{t}") for t in range(PACK)]
+        for s in range(PASSES):
+            layer1_pass(s, prepare_w1(0, s), [banks0], [whole])
+            if s == 0:
+                gather_words(PASSES - 1, reuses="w1_grouped00")
+        weights1 = [prepare_w1(1, 0)]
+        relu0 = tile([P, PACK, S], F32, "relu0")
+        for t in range(PACK):
+            nc.scalar.activation(relu0[:, t, :], banks0[t][:], ACT.Relu)
+        h0_grouped = tile([P, S * PACK], BF16, "h0_grouped")
+        for cols in halves:
+            nc.scalar.activation(*interleaved(h0_grouped[:, PACK * cols.start : PACK * cols.stop], relu0[:, :, cols]), ACT.Square)
+
+        banks1 = [
+            [psum.tile([P, HALF], F32, name=f"bank1{b}{t}", tag=f"b{PACK * (1 - b) + t}") for t in range(PACK)] for b in range(2)
+        ]
+        for s in range(PASSES):
+            if s > 0:
+                weights1.append(prepare_w1(1, s))
+            layer1_pass(s, weights1[s], banks1, halves)
+
+        h0_words = tile([P, S], U32, "h0_words", reuses="w1_grouped12")
+        h0_scales = tile([P, S], U8, "h0_scales")
+        quantize(h0_words, h0_scales, h0_grouped, whole)
+
+        w2_grouped = tile([P, GROUPS * N * PACK], BF16, "w2_grouped")
+        w2_words = tile([P, GROUPS * N], U32, "w2_words", reuses="w1_words12")
+        w2_scales = tile([P, GROUPS * N], U8, "w2_scales")
+        nc.scalar.copy(
+            w2_grouped[:].rearrange("p (g c i j) -> p g c j i", g=GROUPS, i=RUN, j=PACK),
+            w2_raw[:].rearrange("p g j (c i) -> p g c j i", i=RUN),
+        )
+        quantize(w2_words, w2_scales, w2_grouped, slice(0, GROUPS * N))
+
+        relu1 = tile([P, PACK, S], F32, "relu1")
+        h1_grouped = tile([P, S * PACK], BF16, "h1_grouped")
+        h1_words = tile([P, S], U32, "h1_words")
+        h1_scales = tile([P, S], U8, "h1_scales")
+        for b, cols in enumerate(halves):
+            for t in range(PACK):
+                if b == 0 and t >= 2:
+                    nc.vector.tensor_scalar_max(relu1[:, t, cols], banks1[b][t][:], 0.0)
+                else:
+                    nc.scalar.activation(relu1[:, t, cols], banks1[b][t][:], ACT.Relu)
+        for q in range(S // P):
+            dst, src = interleaved(h1_grouped[:, q * P * PACK : (q + 1) * P * PACK], relu1[:, :, q * P : (q + 1) * P])
+            if q % 2 == 0:
                 nc.scalar.activation(dst, src, ACT.Square)
             else:
                 nc.vector.tensor_tensor(dst, src, src, ALU.mult)
 
-        whole = [slice(0, S)]
-        halves = [slice(0, HALF), slice(HALF, S)]
-        banks0 = [[psum.tile([P, S], F32, name=f"bank0{t}", tag=f"b{t}") for t in range(PACK)]]
-        for s in range(PASSES):
-            multiply(s, prepare_w1(0, s), banks0, whole)
-            if s == 0:
-                picked = tile([P, S], U32, "g_words2", tag="w1_00_grouped")
-                nc.vector.tensor_copy(picked[:], words[:].indirect(offs_t[:]))
-                g_words.append(picked)
-        weights = [prepare_w1(1, 0)]
-        r0 = tile([P, PACK, S], F32, "r0")
-        relu(r0, banks0[0], whole[0], RELU0)
-        grouped0 = tile([P, S * PACK], BF16, "h0_grouped")
-        for cols in halves:
-            nc.scalar.activation(
-                grouped0[:, PACK * cols.start : PACK * cols.stop].rearrange("p (c i t) -> p c t i", i=4, t=PACK),
-                r0[:, :, cols].rearrange("p t (c i) -> p c t i", i=4),
-                ACT.Square,
-            )
-        banks1 = [
-            [psum.tile([P, HALF], F32, name=f"bank1{b}{t}", tag=f"b{4 * (1 - b) + t}") for t in range(PACK)] for b in range(2)
-        ]
-        for s in range(PASSES):
-            if s >= len(weights):
-                weights.append(prepare_w1(1, s))
-            multiply(s, weights[s], banks1, halves)
-        codes0 = tile([P, S], U32, "h0_codes", tag="w1_12_grouped")
-        scales0 = tile([P, S], U8, "h0_scales")
-        quantize(codes0, scales0, grouped0, whole[0])
-
-        w2_grouped = tile([P, HALVES * N * PACK], BF16, "w2_grouped")
-        w2_codes = tile([P, HALVES * N], U32, "w2_codes", tag="w1_12_codes")
-        w2_scales = tile([P, HALVES * N], U8, "w2_scales")
-        nc.scalar.copy(
-            w2_grouped[:].rearrange("p (g c i j) -> p g c j i", g=HALVES, i=4, j=PACK),
-            w2_raw[:].rearrange("p g j (c i) -> p g c j i", i=4),
-        )
-        quantize(w2_codes, w2_scales, w2_grouped, slice(0, HALVES * N))
-
-        r1 = tile([P, PACK, S], F32, "r1")
-        grouped1 = tile([P, S * PACK], BF16, "h1_grouped")
-        codes1 = tile([P, S], U32, "h1_codes")
-        scales1 = tile([P, S], U8, "h1_scales")
-        for b in range(2):
-            relu(r1, banks1[b], halves[b], RELU1[b])
-        for q in range(4):
-            square(1, r1, grouped1, q)
-
         y = tile([P, S], F32, "y")
-        first = 0
-        for b, width in enumerate(Y_BLOCKS):
-            cols = slice(first, first + width)
-            first = first + width
-            y_bank = psum.tile([P, width], F32, name=f"y_bank{b}", tag=f"b{4 + b}")
-            quantize(codes1, scales1, grouped1, cols)
-            for h, (codes, scales) in enumerate(((codes0, scales0), (codes1, scales1))):
+        for b, cols in enumerate(Y_BLOCKS):
+            y_bank = psum.tile([P, cols.stop - cols.start], F32, name=f"y_bank{b}", tag=f"b{PACK + b}")
+            quantize(h1_words, h1_scales, h1_grouped, cols)
+            for g, (words, scales) in enumerate(((h0_words, h0_scales), (h1_words, h1_scales))):
                 nc.tensor.matmul_mx(
                     out=y_bank[:],
-                    lhsT=w2_codes[:, h * N : (h + 1) * N].bitcast(FP8X4),
-                    lhsT_scale=w2_scales[:, h * N : (h + 1) * N],
-                    rhs=codes[:, cols].bitcast(FP8X4),
+                    lhsT=w2_words[:, g * N : (g + 1) * N].bitcast(FP8X4),
+                    lhsT_scale=w2_scales[:, g * N : (g + 1) * N],
+                    rhs=words[:, cols].bitcast(FP8X4),
                     rhs_scale=scales[:, cols],
-                    start=(h == 0),
-                    stop=(h == HALVES - 1),
+                    start=(g == 0),
+                    stop=(g == GROUPS - 1),
                 )
-            copy(Y_SCALAR[b], y[:, cols], y_bank[:])
+            copy(b == 0, y[:, cols], y_bank[:])
 
-        prods = [tile([P, V], F32, f"prod{d}") for d in range(D)]
+        terms = [tile([P, V], F32, f"term{d}") for d in range(D)]
         pair = tile([P, V], F32, "pair")
         result = tile([P, V], F32, "result")
         for d in range(D):
-            nc.vector.tensor_tensor(prods[d][:], y[:].indirect(pos_t[d][:]), gate_t[:, d, :], ALU.mult)
+            nc.vector.tensor_tensor(terms[d][:], y[:].indirect(pos_t[d][:]), gate_t[:, d, :], ALU.mult)
         parts = [slice(0, V // 2), slice(V // 2, V)]
         for part in parts:
-            nc.vector.tensor_tensor(pair[:, part], prods[0][:, part], prods[1][:, part], ALU.add)
+            nc.vector.tensor_tensor(pair[:, part], terms[0][:, part], terms[1][:, part], ALU.add)
         for part, queue in zip(parts, (nc.sync, nc.scalar)):
-            nc.vector.tensor_tensor(result[:, part], pair[:, part], prods[2][:, part], ALU.add)
+            nc.vector.tensor_tensor(result[:, part], pair[:, part], terms[2][:, part], ALU.add)
             queue.dma_start(out=out[:, part], in_=result[:, part])

@@ -20,11 +20,11 @@ K_PASS = P * PACK
 PASSES = K // K_PASS
 GROUPS = H // K_PASS
 W = 512
-RUN = 4
+RUN = 8
 HALF = S // 2
 
-X_RUNS_ON_SCALAR = 112
-W1_ROWS_ON_VECTOR = ((32, 32, P), (2 * P, 2 * P, 2 * P))
+X_RUNS_ON_SCALAR = 56
+W1_ROWS_ON_VECTOR = ((32, 32, P), (2 * P, 2 * P, 208))
 Y_BLOCKS = (slice(0, 256), slice(256, 384), slice(384, 512))
 
 
@@ -174,7 +174,7 @@ def tile_picked_sub_mlp_relu2_sub_e_kernel(tc, xT, w1, w2, gate, offs, pos1, pos
         h1_scales = tile([P, S], U8, "h1_scales")
         for b, cols in enumerate(halves):
             for t in range(PACK):
-                if b == 0 and t >= 2:
+                if t >= 2 + b:
                     nc.vector.tensor_scalar_max(relu1[:, t, cols], banks1[b][t][:], 0.0)
                 else:
                     nc.scalar.activation(relu1[:, t, cols], banks1[b][t][:], ACT.Relu)

@@ -24,7 +24,7 @@ RUN = 8
 HALF = S // 2
 
 X_RUNS_ON_SCALAR = 56
-W1_ROWS_ON_VECTOR = ((32, 32, P), (2 * P, 2 * P, 208))
+W1_ROWS_ON_VECTOR = (((0, 0), (0, 32), (P, 0)), ((P, P), (P, P), (P, 64)))
 Y_BLOCKS = (slice(0, 256), slice(256, 384), slice(384, 512))
 
 
@@ -101,45 +101,52 @@ def tile_picked_sub_mlp_relu2_sub_e_kernel(tc, xT, w1, w2, gate, offs, pos1, pos
         picked_scales = tile([P, S], U8, "picked_scales")
         nc.vector.tensor_copy(picked_scales[:], x_scales[:].indirect(offs_t[:]))
 
-        def prepare_w1(g, s):
-            grouped = tile([P, W * PACK], BF16, f"w1_grouped{g}{s}")
-            words = tile([P, W], U32, f"w1_words{g}{s}")
-            scales = tile([P, W], U8, f"w1_scales{g}{s}")
+        def round_w1(g, s):
             src = w1_raw[g][s][:].rearrange("p j (m u e) -> p u m j e", u=2, e=2)
-            dst = grouped[:].rearrange("p (u e m j) -> p u m j e", u=2, e=2, j=PACK)
+            pairs = []
             for u in range(2):
-                cut = min(max(W1_ROWS_ON_VECTOR[g][s] - u * P, 0), P)
+                grouped = tile([P, 2 * P * PACK], BF16, f"w1_grouped{g}{s}{u}")
+                dst = grouped[:].rearrange("p (e m j) -> p m j e", e=2, j=PACK)
+                cut = W1_ROWS_ON_VECTOR[g][s][u]
                 if cut > 0:
-                    copy(False, dst[:, u, :cut], src[:, u, :cut])
+                    copy(False, dst[:, :cut], src[:, u, :cut])
                 if cut < P:
-                    copy(True, dst[:, u, cut:], src[:, u, cut:])
-            for u in range(2):
-                quantize(words, scales, grouped, slice(2 * u * P, 2 * (u + 1) * P))
+                    copy(True, dst[:, cut:], src[:, u, cut:])
+                pairs.append(grouped)
+            return pairs
+
+        def quantize_w1(g, s, u, grouped, reuses=None):
+            words = tile([P, 2 * P], U32, f"w1_words{g}{s}{u}", reuses)
+            scales = tile([P, 2 * P], U8, f"w1_scales{g}{s}{u}")
+            quantize(words, scales, grouped, slice(0, 2 * P))
             return words, scales
 
         def layer1_pass(s, weights, banks, blocks):
-            words, scales = weights
             for block_banks, cols in zip(banks, blocks):
-                for t in range(PACK):
-                    nc.tensor.matmul_mx(
-                        out=block_banks[t][:],
-                        lhsT=words[:, t * P : (t + 1) * P].bitcast(FP8X4),
-                        lhsT_scale=scales[:, t * P : (t + 1) * P],
-                        rhs=picked_words[s][:, cols].bitcast(FP8X4),
-                        rhs_scale=picked_scales[4 * s : P, cols],
-                        start=(s == 0),
-                        stop=(s == PASSES - 1),
-                    )
+                for u, (words, scales) in weights.items():
+                    for e in range(2):
+                        nc.tensor.matmul_mx(
+                            out=block_banks[2 * u + e][:],
+                            lhsT=words[:, e * P : (e + 1) * P].bitcast(FP8X4),
+                            lhsT_scale=scales[:, e * P : (e + 1) * P],
+                            rhs=picked_words[s][:, cols].bitcast(FP8X4),
+                            rhs_scale=picked_scales[4 * s : P, cols],
+                            start=(s == 0),
+                            stop=(s == PASSES - 1),
+                        )
+
+        def quantize_piece(g, s, pairs):
+            return {u: quantize_w1(g, s, u, pairs[u]) for u in range(2)}
 
         whole = slice(0, S)
         halves = [slice(0, HALF), slice(HALF, S)]
 
         banks0 = [psum.tile([P, S], F32, name=f"bank0{t}", tag=f"b{t}") for t in range(PACK)]
-        for s in range(PASSES):
-            layer1_pass(s, prepare_w1(0, s), [banks0], [whole])
-            if s == 0:
-                gather_words(PASSES - 1, reuses="w1_grouped00")
-        weights1 = [prepare_w1(1, 0)]
+        layer1_pass(0, quantize_piece(0, 0, round_w1(0, 0)), [banks0], [whole])
+        gather_words(PASSES - 1, reuses="w1_grouped000")
+        for s in range(1, PASSES):
+            layer1_pass(s, quantize_piece(0, s, round_w1(0, s)), [banks0], [whole])
+        weights1 = [quantize_piece(1, 0, round_w1(1, 0))]
         relu0 = tile([P, PACK, S], F32, "relu0")
         for t in range(PACK):
             nc.scalar.activation(relu0[:, t, :], banks0[t][:], ACT.Relu)
@@ -152,15 +159,15 @@ def tile_picked_sub_mlp_relu2_sub_e_kernel(tc, xT, w1, w2, gate, offs, pos1, pos
         ]
         for s in range(PASSES):
             if s > 0:
-                weights1.append(prepare_w1(1, s))
+                weights1.append(quantize_piece(1, s, round_w1(1, s)))
             layer1_pass(s, weights1[s], banks1, halves)
 
-        h0_words = tile([P, S], U32, "h0_words", reuses="w1_grouped12")
+        h0_words = tile([P, S], U32, "h0_words", reuses="w1_grouped121")
         h0_scales = tile([P, S], U8, "h0_scales")
         quantize(h0_words, h0_scales, h0_grouped, whole)
 
         w2_grouped = tile([P, GROUPS * N * PACK], BF16, "w2_grouped")
-        w2_words = tile([P, GROUPS * N], U32, "w2_words", reuses="w1_words12")
+        w2_words = tile([P, GROUPS * N], U32, "w2_words", reuses="w1_words121")
         w2_scales = tile([P, GROUPS * N], U8, "w2_scales")
         nc.scalar.copy(
             w2_grouped[:].rearrange("p (g c i j) -> p g c j i", g=GROUPS, i=RUN, j=PACK),
@@ -189,12 +196,12 @@ def tile_picked_sub_mlp_relu2_sub_e_kernel(tc, xT, w1, w2, gate, offs, pos1, pos
         for b, cols in enumerate(Y_BLOCKS):
             y_bank = psum.tile([P, cols.stop - cols.start], F32, name=f"y_bank{b}", tag=f"b{PACK + b}")
             quantize(h1_words, h1_scales, h1_grouped, cols)
-            for g, (words, scales) in enumerate(((h0_words, h0_scales), (h1_words, h1_scales))):
+            for g, (words, scales) in enumerate(((h0_words[:, cols], h0_scales), (h1_words[:, cols], h1_scales))):
                 nc.tensor.matmul_mx(
                     out=y_bank[:],
                     lhsT=w2_words[:, g * N : (g + 1) * N].bitcast(FP8X4),
                     lhsT_scale=w2_scales[:, g * N : (g + 1) * N],
-                    rhs=words[:, cols].bitcast(FP8X4),
+                    rhs=words.bitcast(FP8X4),
                     rhs_scale=scales[:, cols],
                     start=(g == 0),
                     stop=(g == GROUPS - 1),

@@ -154,13 +154,22 @@ def tile_picked_sub_mlp_relu2_sub_e_kernel(tc, xT, w1, w2, gate, offs, pos1, pos
         for cols in halves:
             nc.scalar.activation(*interleaved(h0_grouped[:, PACK * cols.start : PACK * cols.stop], relu0[:, :, cols]), ACT.Square)
 
-        banks1 = [
-            [psum.tile([P, HALF], F32, name=f"bank1{b}{t}", tag=f"b{PACK * (1 - b) + t}") for t in range(PACK)] for b in range(2)
-        ]
+        banks1 = [[psum.tile([P, 2, HALF], F32, name=f"bank1{h}{u}", tag=f"b{PACK + 2 * h + u}") for u in range(2)] for h in range(2)]
         for s in range(PASSES):
             if s > 0:
                 weights1.append(quantize_piece(1, s, round_w1(1, s)))
-            layer1_pass(s, weights1[s], banks1, halves)
+            for h, cols in enumerate(halves):
+                for u, (words, scales) in weights1[s].items():
+                    for e in range(2):
+                        nc.tensor.matmul_mx(
+                            out=banks1[h][u][:, e, :],
+                            lhsT=words[:, e * P : (e + 1) * P].bitcast(FP8X4),
+                            lhsT_scale=scales[:, e * P : (e + 1) * P],
+                            rhs=picked_words[s][:, cols].bitcast(FP8X4),
+                            rhs_scale=picked_scales[4 * s : P, cols],
+                            start=(s == 0 and e == 0),
+                            stop=(s == PASSES - 1 and e == 1),
+                        )
 
         h0_words = tile([P, S], U32, "h0_words", reuses="w1_grouped121")
         h0_scales = tile([P, S], U8, "h0_scales")
@@ -173,18 +182,17 @@ def tile_picked_sub_mlp_relu2_sub_e_kernel(tc, xT, w1, w2, gate, offs, pos1, pos
             w2_grouped[:].rearrange("p (g c i j) -> p g c j i", g=GROUPS, i=RUN, j=PACK),
             w2_raw[:].rearrange("p g j (c i) -> p g c j i", i=RUN),
         )
-        quantize(w2_words, w2_scales, w2_grouped, slice(0, GROUPS * N))
 
         relu1 = tile([P, PACK, S], F32, "relu1")
         h1_grouped = tile([P, S * PACK], BF16, "h1_grouped")
         h1_words = tile([P, S], U32, "h1_words")
         h1_scales = tile([P, S], U8, "h1_scales")
-        for b, cols in enumerate(halves):
-            for t in range(PACK):
-                if t >= 2 + b:
-                    nc.vector.tensor_scalar_max(relu1[:, t, cols], banks1[b][t][:], 0.0)
-                else:
-                    nc.scalar.activation(relu1[:, t, cols], banks1[b][t][:], ACT.Relu)
+        nc.vector.tensor_scalar_max(relu1[:, 2:4, halves[0]], banks1[0][1][:], 0.0)
+        nc.scalar.activation(relu1[:, 0:2, halves[0]], banks1[0][0][:], ACT.Relu)
+        nc.vector.tensor_scalar_max(relu1[:, 3, halves[1]], banks1[1][1][:, 1, :], 0.0)
+        nc.scalar.activation(relu1[:, 0:2, halves[1]], banks1[1][0][:], ACT.Relu)
+        nc.scalar.activation(relu1[:, 2, halves[1]], banks1[1][1][:, 0, :], ACT.Relu)
+        quantize(w2_words, w2_scales, w2_grouped, slice(0, GROUPS * N))
         for q in range(S // P):
             dst, src = interleaved(h1_grouped[:, q * P * PACK : (q + 1) * P * PACK], relu1[:, :, q * P : (q + 1) * P])
             if q % 2 == 0:
@@ -194,7 +202,7 @@ def tile_picked_sub_mlp_relu2_sub_e_kernel(tc, xT, w1, w2, gate, offs, pos1, pos
 
         y = tile([P, S], F32, "y")
         for b, cols in enumerate(Y_BLOCKS):
-            y_bank = psum.tile([P, cols.stop - cols.start], F32, name=f"y_bank{b}", tag=f"b{PACK + b}")
+            y_bank = psum.tile([P, cols.stop - cols.start], F32, name=f"y_bank{b}", tag=f"b{b}")
             quantize(h1_words, h1_scales, h1_grouped, cols)
             for g, (words, scales) in enumerate(((h0_words[:, cols], h0_scales), (h1_words[:, cols], h1_scales))):
                 nc.tensor.matmul_mx(

@@ -24,7 +24,7 @@ RUN = 8
 HALF = S // 2
 
 X_RUNS_ON_SCALAR = 56
-W1_ROWS_ON_VECTOR = (((0, 0), (0, 32), (P, 0)), ((P, P), (P, P), (P, 64)))
+W1_ROWS_ON_VECTOR = (((0, 0), (P, 0), (P, 48)), ((P, P), (P, P), (P, 64)))
 Y_BLOCKS = (slice(0, 256), slice(256, 384), slice(384, 512))
 
 
@@ -58,8 +58,6 @@ def tile_picked_sub_mlp_relu2_sub_e_kernel(tc, xT, w1, w2, gate, offs, pos1, pos
 
         offs_t = keep.tile([P, S // 16], U16, name="offs_t")
         pos_t = [keep.tile([P, V // 16], U16, name=f"pos{d}_t") for d in range(D)]
-        x_scales = tile([P, T], U8, "x_scales")
-        nc.gpsimd.memset(x_scales[:], 0)
 
         def load_rows(name, source, s, first, width):
             raw = tile([P, PACK, width], F32, name)
@@ -67,9 +65,15 @@ def tile_picked_sub_mlp_relu2_sub_e_kernel(tc, xT, w1, w2, gate, offs, pos1, pos
             nc.sync.dma_start(out=raw[:], in_=rows.rearrange("(p j) w -> p j w", j=PACK))
             return raw
 
-        x_raw = [load_rows("x_raw0", xT, 0, 0, T)]
+        def load_x(s, half):
+            raw = tile([P, 2, T], F32, f"x_raw{s}{half}")
+            rows = xT[s * K_PASS : (s + 1) * K_PASS, :].rearrange("(p j) w -> p j w", j=PACK)
+            nc.sync.dma_start(out=raw[:], in_=rows[:, 2 * half : 2 * half + 2, :])
+            return raw
+
+        x_raw = [load_x(0, 0)]
         nc.sync.dma_start(offs_t[:], offs)
-        x_raw.extend(load_rows(f"x_raw{s}", xT, s, 0, T) for s in range(1, PASSES))
+        x_raw.extend(load_x(n // 2, n % 2) for n in range(1, 2 * PASSES))
         w1_raw = [[load_rows(f"w1_raw{g}{s}", w1, s, g * W, W) for s in range(PASSES)] for g in range(GROUPS)]
         w2_raw = tile([P, GROUPS, PACK, N], F32, "w2_raw")
         nc.sync.dma_start(out=w2_raw[:], in_=w2.rearrange("(g p j) m -> p g j m", p=P, j=PACK))
@@ -78,28 +82,22 @@ def tile_picked_sub_mlp_relu2_sub_e_kernel(tc, xT, w1, w2, gate, offs, pos1, pos
         for d, pos in enumerate((pos1, pos2, pos3)):
             nc.sync.dma_start(pos_t[d][:], pos)
 
-        x_words, picked_words = [], []
-
-        def gather_words(s, reuses=None):
-            picked = tile([P, S], U32, f"picked_words{s}", reuses)
-            nc.vector.tensor_copy(picked[:], x_words[s][:].indirect(offs_t[:]))
-            picked_words.append(picked)
-
-        chunks = [slice(0, W), slice(W, T)]
+        picked_words, picked_scales = [], []
         for s in range(PASSES):
-            words = tile([P, T], U32, f"x_words{s}")
-            grouped = tile([P, T * PACK], BF16, f"x_grouped{s}")
-            copy(False, *interleaved(grouped[:, : W * PACK], x_raw[s][:, :, chunks[0]]))
-            dst, src = interleaved(grouped[:, W * PACK :], x_raw[s][:, :, chunks[1]])
-            copy(True, dst[:, :X_RUNS_ON_SCALAR], src[:, :X_RUNS_ON_SCALAR])
-            copy(False, dst[:, X_RUNS_ON_SCALAR:], src[:, X_RUNS_ON_SCALAR:])
-            for cols in chunks:
-                quantize(words, x_scales, grouped, cols, scale_row=4 * s)
-            x_words.append(words)
-            if s < PASSES - 1:
-                gather_words(s)
-        picked_scales = tile([P, S], U8, "picked_scales")
-        nc.vector.tensor_copy(picked_scales[:], x_scales[:].indirect(offs_t[:]))
+            planes = tile([P, PACK, S], F32, f"planes{s}")
+            for j in range(PACK):
+                window = x_raw[2 * s + j // 2][:, j % 2, :].indirect(offs_t[:])
+                if j < PACK - 1:
+                    nc.scalar.activation(planes[:, j, :], window, ACT.Copy)
+                else:
+                    nc.vector.tensor_copy(planes[:, j, :], window)
+            grouped = tile([P, S * PACK], BF16, f"x_grouped{s}")
+            copy(False, *interleaved(grouped[:], planes[:]))
+            words = tile([P, S], U32, f"picked_words{s}")
+            scales = tile([P, S], U8, f"picked_scales{s}")
+            quantize(words, scales, grouped, slice(0, S))
+            picked_words.append(words)
+            picked_scales.append(scales)
 
         def round_w1(g, s):
             src = w1_raw[g][s][:].rearrange("p j (m u e) -> p u m j e", u=2, e=2)
@@ -130,7 +128,7 @@ def tile_picked_sub_mlp_relu2_sub_e_kernel(tc, xT, w1, w2, gate, offs, pos1, pos
                             lhsT=words[:, e * P : (e + 1) * P].bitcast(FP8X4),
                             lhsT_scale=scales[:, e * P : (e + 1) * P],
                             rhs=picked_words[s][:, cols].bitcast(FP8X4),
-                            rhs_scale=picked_scales[4 * s : P, cols],
+                            rhs_scale=picked_scales[s][:, cols],
                             start=(s == 0),
                             stop=(s == PASSES - 1),
                         )
@@ -142,14 +140,13 @@ def tile_picked_sub_mlp_relu2_sub_e_kernel(tc, xT, w1, w2, gate, offs, pos1, pos
         halves = [slice(0, HALF), slice(HALF, S)]
 
         banks0 = [psum.tile([P, S], F32, name=f"bank0{t}", tag=f"b{t}") for t in range(PACK)]
-        layer1_pass(0, quantize_piece(0, 0, round_w1(0, 0)), [banks0], [whole])
-        gather_words(PASSES - 1, reuses="w1_grouped000")
-        for s in range(1, PASSES):
+        for s in range(PASSES):
             layer1_pass(s, quantize_piece(0, s, round_w1(0, s)), [banks0], [whole])
-        weights1 = [quantize_piece(1, 0, round_w1(1, 0))]
         relu0 = tile([P, PACK, S], F32, "relu0")
-        for t in range(PACK):
+        nc.vector.tensor_scalar_max(relu0[:, 1, :], banks0[1][:], 0.0)
+        for t in (0, 2, 3):
             nc.scalar.activation(relu0[:, t, :], banks0[t][:], ACT.Relu)
+        weights1 = [quantize_piece(1, 0, round_w1(1, 0))]
         h0_grouped = tile([P, S * PACK], BF16, "h0_grouped")
         for cols in halves:
             nc.scalar.activation(*interleaved(h0_grouped[:, PACK * cols.start : PACK * cols.stop], relu0[:, :, cols]), ACT.Square)
@@ -166,7 +163,7 @@ def tile_picked_sub_mlp_relu2_sub_e_kernel(tc, xT, w1, w2, gate, offs, pos1, pos
                             lhsT=words[:, e * P : (e + 1) * P].bitcast(FP8X4),
                             lhsT_scale=scales[:, e * P : (e + 1) * P],
                             rhs=picked_words[s][:, cols].bitcast(FP8X4),
-                            rhs_scale=picked_scales[4 * s : P, cols],
+                            rhs_scale=picked_scales[s][:, cols],
                             start=(s == 0 and e == 0),
                             stop=(s == PASSES - 1 and e == 1),
                         )
@@ -219,8 +216,11 @@ def tile_picked_sub_mlp_relu2_sub_e_kernel(tc, xT, w1, w2, gate, offs, pos1, pos
         terms = [tile([P, V], F32, f"term{d}") for d in range(D)]
         pair = tile([P, V], F32, "pair")
         result = tile([P, V], F32, "result")
-        for d in range(D):
+        fetched = tile([P, V], F32, "fetched")
+        nc.scalar.activation(fetched[:], y[:].indirect(pos_t[D - 1][:]), ACT.Copy)
+        for d in range(D - 1):
             nc.vector.tensor_tensor(terms[d][:], y[:].indirect(pos_t[d][:]), gate_t[:, d, :], ALU.mult)
+        nc.vector.tensor_tensor(terms[D - 1][:], fetched[:], gate_t[:, D - 1, :], ALU.mult)
         parts = [slice(0, V // 2), slice(V // 2, V)]
         for part in parts:
             nc.vector.tensor_tensor(pair[:, part], terms[0][:, part], terms[1][:, part], ALU.add)

@@ -24,7 +24,7 @@ RUN = 8
 HALF = S // 2
 
 X_RUNS_ON_SCALAR = 56
-W1_ROWS_ON_VECTOR = (((0, 0), (P, 0), (P, 48)), ((P, P), (P, P), (P, 64)))
+W1_ROWS_ON_VECTOR = (((0, 0), (P, 0), (P, 48)), ((P, P), (P, P), (P, 48)))
 Y_BLOCKS = (slice(0, 256), slice(256, 384), slice(384, 512))
 
 
@@ -75,8 +75,7 @@ def tile_picked_sub_mlp_relu2_sub_e_kernel(tc, xT, w1, w2, gate, offs, pos1, pos
         nc.sync.dma_start(offs_t[:], offs)
         x_raw.extend(load_x(n // 2, n % 2) for n in range(1, 2 * PASSES))
         w1_raw = [[load_rows(f"w1_raw{g}{s}", w1, s, g * W, W) for s in range(PASSES)] for g in range(GROUPS)]
-        w2_raw = tile([P, GROUPS, PACK, N], F32, "w2_raw")
-        nc.sync.dma_start(out=w2_raw[:], in_=w2.rearrange("(g p j) m -> p g j m", p=P, j=PACK))
+        w2_raw = [load_rows(f"w2_raw{g}", w2, g, 0, N) for g in range(GROUPS)]
         gate_t = tile([P, D, V], F32, "gate_t")
         nc.sync.dma_start(out=gate_t[:], in_=gate.rearrange("d m v -> m d v"))
         for d, pos in enumerate((pos1, pos2, pos3)):
@@ -143,8 +142,8 @@ def tile_picked_sub_mlp_relu2_sub_e_kernel(tc, xT, w1, w2, gate, offs, pos1, pos
         for s in range(PASSES):
             layer1_pass(s, quantize_piece(0, s, round_w1(0, s)), [banks0], [whole])
         relu0 = tile([P, PACK, S], F32, "relu0")
-        nc.vector.tensor_scalar_max(relu0[:, 1, :], banks0[1][:], 0.0)
-        for t in (0, 2, 3):
+        nc.vector.tensor_scalar_max(relu0[:, 0, :], banks0[0][:], 0.0)
+        for t in (1, 2, 3):
             nc.scalar.activation(relu0[:, t, :], banks0[t][:], ACT.Relu)
         weights1 = [quantize_piece(1, 0, round_w1(1, 0))]
         h0_grouped = tile([P, S * PACK], BF16, "h0_grouped")
@@ -175,23 +174,26 @@ def tile_picked_sub_mlp_relu2_sub_e_kernel(tc, xT, w1, w2, gate, offs, pos1, pos
         w2_grouped = tile([P, GROUPS * N * PACK], BF16, "w2_grouped")
         w2_words = tile([P, GROUPS * N], U32, "w2_words", reuses="w1_words121")
         w2_scales = tile([P, GROUPS * N], U8, "w2_scales")
-        nc.scalar.copy(
-            w2_grouped[:].rearrange("p (g c i j) -> p g c j i", g=GROUPS, i=RUN, j=PACK),
-            w2_raw[:].rearrange("p g j (c i) -> p g c j i", i=RUN),
-        )
+        for g in range(GROUPS):
+            copy(True, *interleaved(w2_grouped[:, g * N * PACK : (g + 1) * N * PACK], w2_raw[g][:]))
 
-        relu1 = tile([P, PACK, S], F32, "relu1")
         h1_grouped = tile([P, S * PACK], BF16, "h1_grouped")
         h1_words = tile([P, S], U32, "h1_words")
         h1_scales = tile([P, S], U8, "h1_scales")
-        nc.vector.tensor_scalar_max(relu1[:, 2:4, halves[0]], banks1[0][1][:], 0.0)
-        nc.scalar.activation(relu1[:, 0:2, halves[0]], banks1[0][0][:], ACT.Relu)
-        nc.vector.tensor_scalar_max(relu1[:, 3, halves[1]], banks1[1][1][:, 1, :], 0.0)
-        nc.scalar.activation(relu1[:, 0:2, halves[1]], banks1[1][0][:], ACT.Relu)
-        nc.scalar.activation(relu1[:, 2, halves[1]], banks1[1][1][:, 0, :], ACT.Relu)
+        both = tile([P, 2, S, 2], F32, "relu1")
+
+        def woven(h, u, nodes):
+            cols = slice(h * HALF + nodes.start, h * HALF + nodes.stop)
+            return both[:, u, cols, :], banks1[h][u][:, :, nodes].rearrange("p e n -> p n e")
+
+        nc.vector.tensor_scalar_max(*woven(0, 1, halves[0]), 0.0)
+        nc.scalar.activation(*woven(0, 0, halves[0]), ACT.Relu)
+        nc.scalar.activation(*woven(1, 0, halves[0]), ACT.Relu)
+        nc.scalar.activation(*woven(1, 1, halves[0]), ACT.Relu)
         quantize(w2_words, w2_scales, w2_grouped, slice(0, GROUPS * N))
         for q in range(S // P):
-            dst, src = interleaved(h1_grouped[:, q * P * PACK : (q + 1) * P * PACK], relu1[:, :, q * P : (q + 1) * P])
+            dst = h1_grouped[:, q * P * PACK : (q + 1) * P * PACK].rearrange("p (n u e) -> p n u e", u=2, e=2)
+            src = both[:, :, q * P : (q + 1) * P, :].rearrange("p u n e -> p n u e")
             if q % 2 == 0:
                 nc.scalar.activation(dst, src, ACT.Square)
             else:
@@ -211,7 +213,7 @@ def tile_picked_sub_mlp_relu2_sub_e_kernel(tc, xT, w1, w2, gate, offs, pos1, pos
                     start=(g == 0),
                     stop=(g == GROUPS - 1),
                 )
-            copy(b == 0, y[:, cols], y_bank[:])
+            copy(b != 1, y[:, cols], y_bank[:])
 
         terms = [tile([P, V], F32, f"term{d}") for d in range(D)]
         pair = tile([P, V], F32, "pair")

@@ -154,6 +154,10 @@ def tile_picked_sub_mlp_relu2_sub_e_kernel(tc, xT, w1, w2, gate, offs, pos1, pos
         for s in range(PASSES):
             if s > 0:
                 weights1.append(quantize_piece(1, s, round_w1(1, s)))
+            if s == 1:
+                h0_words = tile([P, HALF], U32, "h0_words", reuses="w1_grouped111")
+                h0_scales = tile([P, HALF], U8, "h0_scales")
+                quantize(h0_words, h0_scales, h0_grouped, halves[0])
             for h, cols in enumerate(halves):
                 for u, (words, scales) in weights1[s].items():
                     for e in range(2):
@@ -167,12 +171,12 @@ def tile_picked_sub_mlp_relu2_sub_e_kernel(tc, xT, w1, w2, gate, offs, pos1, pos
                             stop=(s == PASSES - 1 and e == 1),
                         )
 
-        h0_words = tile([P, S], U32, "h0_words", reuses="w1_grouped121")
-        h0_scales = tile([P, S], U8, "h0_scales")
-        quantize(h0_words, h0_scales, h0_grouped, whole)
+        late_words = tile([P, HALF], U32, "h0_late_words", reuses="w1_grouped121")
+        late_scales = tile([P, HALF], U8, "h0_late_scales")
+        quantize(late_words, late_scales, h0_grouped[:, HALF * PACK :], halves[0])
 
         w2_grouped = tile([P, GROUPS * N * PACK], BF16, "w2_grouped")
-        w2_words = tile([P, GROUPS * N], U32, "w2_words", reuses="w1_words121")
+        w2_words = tile([P, GROUPS * N], U32, "w2_words")
         w2_scales = tile([P, GROUPS * N], U8, "w2_scales")
         for g in range(GROUPS):
             copy(True, *interleaved(w2_grouped[:, g * N * PACK : (g + 1) * N * PACK], w2_raw[g][:]))
@@ -203,13 +207,15 @@ def tile_picked_sub_mlp_relu2_sub_e_kernel(tc, xT, w1, w2, gate, offs, pos1, pos
         for b, cols in enumerate(Y_BLOCKS):
             y_bank = psum.tile([P, cols.stop - cols.start], F32, name=f"y_bank{b}", tag=f"b{b}")
             quantize(h1_words, h1_scales, h1_grouped, cols)
-            for g, (words, scales) in enumerate(((h0_words[:, cols], h0_scales), (h1_words[:, cols], h1_scales))):
+            late = slice(cols.start - HALF, cols.stop - HALF)
+            first = (h0_words[:, cols], h0_scales[:, cols]) if b == 0 else (late_words[:, late], late_scales[:, late])
+            for g, (words, scales) in enumerate((first, (h1_words[:, cols], h1_scales[:, cols]))):
                 nc.tensor.matmul_mx(
                     out=y_bank[:],
                     lhsT=w2_words[:, g * N : (g + 1) * N].bitcast(FP8X4),
                     lhsT_scale=w2_scales[:, g * N : (g + 1) * N],
                     rhs=words.bitcast(FP8X4),
-                    rhs_scale=scales[:, cols],
+                    rhs_scale=scales,
                     start=(g == 0),
                     stop=(g == GROUPS - 1),
                 )

@@ -176,7 +176,7 @@ def tile_picked_sub_mlp_relu2_sub_e_kernel(tc, xT, w1, w2, gate, offs, pos1, pos
         quantize(late_words, late_scales, h0_grouped[:, HALF * PACK :], halves[0])
 
         w2_grouped = tile([P, GROUPS * N * PACK], BF16, "w2_grouped")
-        w2_words = tile([P, GROUPS * N], U32, "w2_words")
+        w2_words = tile([P, GROUPS * N], U32, "w2_words", reuses="w1_words121")
         w2_scales = tile([P, GROUPS * N], U8, "w2_scales")
         for g in range(GROUPS):
             copy(True, *interleaved(w2_grouped[:, g * N * PACK : (g + 1) * N * PACK], w2_raw[g][:]))
@@ -219,16 +219,20 @@ def tile_picked_sub_mlp_relu2_sub_e_kernel(tc, xT, w1, w2, gate, offs, pos1, pos
                     start=(g == 0),
                     stop=(g == GROUPS - 1),
                 )
-            copy(b != 1, y[:, cols], y_bank[:])
+            copy(True, y[:, cols], y_bank[:])
 
         terms = [tile([P, V], F32, f"term{d}") for d in range(D)]
         pair = tile([P, V], F32, "pair")
         result = tile([P, V], F32, "result")
+        low, high = slice(0, V // 2), slice(V // 2, V)
         fetched = tile([P, V], F32, "fetched")
-        nc.scalar.activation(fetched[:], y[:].indirect(pos_t[D - 1][:]), ACT.Copy)
-        for d in range(D - 1):
-            nc.vector.tensor_tensor(terms[d][:], y[:].indirect(pos_t[d][:]), gate_t[:, d, :], ALU.mult)
-        nc.vector.tensor_tensor(terms[D - 1][:], fetched[:], gate_t[:, D - 1, :], ALU.mult)
+        fetched_high = tile([P, V // 2], F32, "fetched_high")
+        nc.scalar.activation(fetched[:], y[:].indirect(pos_t[2][:]), ACT.Copy)
+        nc.scalar.activation(fetched_high[:], y[:].indirect(pos_t[1][:, V // 32 :]), ACT.Copy)
+        nc.vector.tensor_tensor(terms[0][:], y[:].indirect(pos_t[0][:]), gate_t[:, 0, :], ALU.mult)
+        nc.vector.tensor_tensor(terms[1][:, low], y[:].indirect(pos_t[1][:, : V // 32]), gate_t[:, 1, low], ALU.mult)
+        nc.vector.tensor_tensor(terms[2][:], fetched[:], gate_t[:, 2, :], ALU.mult)
+        nc.vector.tensor_tensor(terms[1][:, high], fetched_high[:], gate_t[:, 1, high], ALU.mult)
         parts = [slice(0, V // 2), slice(V // 2, V)]
         for part in parts:
             nc.vector.tensor_tensor(pair[:, part], terms[0][:, part], terms[1][:, part], ALU.add)

@@ -24,7 +24,8 @@ RUN = 8
 HALF = S // 2
 
 X_RUNS_ON_SCALAR = 56
-W1_ROWS_ON_VECTOR = (((0, 0), (P, 0), (P, 48)), ((P, P), (P, P), (P, 48)))
+W1_ROWS_ON_VECTOR = (((0, 0), (P, 0), (P, 48)), ((P, P), (P, P), (88, 80)))
+W2_RUNS_ON_SCALAR = 8
 Y_BLOCKS = (slice(0, 256), slice(256, 384), slice(384, 512))
 
 
@@ -178,8 +179,10 @@ def tile_picked_sub_mlp_relu2_sub_e_kernel(tc, xT, w1, w2, gate, offs, pos1, pos
         w2_grouped = tile([P, GROUPS * N * PACK], BF16, "w2_grouped")
         w2_words = tile([P, GROUPS * N], U32, "w2_words", reuses="w1_words121")
         w2_scales = tile([P, GROUPS * N], U8, "w2_scales")
-        for g in range(GROUPS):
-            copy(True, *interleaved(w2_grouped[:, g * N * PACK : (g + 1) * N * PACK], w2_raw[g][:]))
+        copy(True, *interleaved(w2_grouped[:, : N * PACK], w2_raw[0][:]))
+        dst, src = interleaved(w2_grouped[:, N * PACK :], w2_raw[1][:])
+        copy(True, dst[:, :W2_RUNS_ON_SCALAR], src[:, :W2_RUNS_ON_SCALAR])
+        copy(False, dst[:, W2_RUNS_ON_SCALAR:], src[:, W2_RUNS_ON_SCALAR:])
 
         h1_grouped = tile([P, S * PACK], BF16, "h1_grouped")
         h1_words = tile([P, S], U32, "h1_words")

@@ -159,8 +159,8 @@ def tile_picked_sub_mlp_relu2_sub_e_kernel(tc, xT, w1, w2, gate, offs, pos1, pos
                 h0_words = tile([P, HALF], U32, "h0_words", reuses="w1_grouped111")
                 h0_scales = tile([P, HALF], U8, "h0_scales")
                 quantize(h0_words, h0_scales, h0_grouped, halves[0])
-            for h, cols in enumerate(halves):
-                for u, (words, scales) in weights1[s].items():
+            for u, (words, scales) in weights1[s].items():
+                for h, cols in enumerate(halves):
                     for e in range(2):
                         nc.tensor.matmul_mx(
                             out=banks1[h][u][:, e, :],
@@ -193,9 +193,9 @@ def tile_picked_sub_mlp_relu2_sub_e_kernel(tc, xT, w1, w2, gate, offs, pos1, pos
             cols = slice(h * HALF + nodes.start, h * HALF + nodes.stop)
             return both[:, u, cols, :], banks1[h][u][:, :, nodes].rearrange("p e n -> p n e")
 
-        nc.vector.tensor_scalar_max(*woven(0, 1, halves[0]), 0.0)
         nc.scalar.activation(*woven(0, 0, halves[0]), ACT.Relu)
-        nc.scalar.activation(*woven(1, 0, halves[0]), ACT.Relu)
+        nc.vector.tensor_scalar_max(*woven(1, 0, halves[0]), 0.0)
+        nc.scalar.activation(*woven(0, 1, halves[0]), ACT.Relu)
         nc.scalar.activation(*woven(1, 1, halves[0]), ACT.Relu)
         quantize(w2_words, w2_scales, w2_grouped, slice(0, GROUPS * N))
         for q in range(S // P):

@@ -23,9 +23,12 @@ W = 512
 RUN = 8
 HALF = S // 2
 
-X_RUNS_ON_SCALAR = 56
-W1_ROWS_ON_VECTOR = (((0, 0), (P, 0), (P, 48)), ((P, P), (P, P), (88, 80)))
-W2_RUNS_ON_SCALAR = 8
+X_RUNS_ON_VECTOR = (64, 64, 44)
+X_NODES_ON_SCALAR = ((S, S, 0, 0), (S, S, S, 0), (S, 384, S, 0))
+WHOLE = 1
+ORDER = (1, 0, 2)
+W1_ROWS_ON_VECTOR = (((0, 64), (P, 0), (64, 72)), ((P, P), (P, 64), (P, P)))
+W2_RUNS_ON_SCALAR = 0
 Y_BLOCKS = (slice(0, 256), slice(256, 384), slice(384, 512))
 
 
@@ -72,35 +75,50 @@ def tile_picked_sub_mlp_relu2_sub_e_kernel(tc, xT, w1, w2, gate, offs, pos1, pos
             nc.sync.dma_start(out=raw[:], in_=rows[:, 2 * half : 2 * half + 2, :])
             return raw
 
-        x_raw = [load_x(0, 0)]
+        w1_whole = load_rows("w1_whole", w1, WHOLE, 0, H)
         nc.sync.dma_start(offs_t[:], offs)
-        x_raw.extend(load_x(n // 2, n % 2) for n in range(1, 2 * PASSES))
-        w1_raw = [[load_rows(f"w1_raw{g}{s}", w1, s, g * W, W) for s in range(PASSES)] for g in range(GROUPS)]
+        x_whole = load_rows("x_raw0", xT, 0, 0, T)
+        x_raw = [load_x(1 + n // 2, n % 2) for n in range(4)]
+        x_planes = [
+            [x_whole[:, j, :] for j in range(PACK)],
+            [x_raw[j // 2][:, j % 2, :] for j in range(PACK)],
+            [x_raw[2 + j // 2][:, j % 2, :] for j in range(PACK)],
+        ]
+        w1_raw = [
+            {s: w1_whole[:, :, g * W : (g + 1) * W] if s == WHOLE else load_rows(f"w1_raw{g}{s}", w1, s, g * W, W)[:] for s in ORDER}
+            for g in range(GROUPS)
+        ]
         w2_raw = [load_rows(f"w2_raw{g}", w2, g, 0, N) for g in range(GROUPS)]
         gate_t = tile([P, D, V], F32, "gate_t")
         nc.sync.dma_start(out=gate_t[:], in_=gate.rearrange("d m v -> m d v"))
         for d, pos in enumerate((pos1, pos2, pos3)):
             nc.sync.dma_start(pos_t[d][:], pos)
 
-        picked_words, picked_scales = [], []
-        for s in range(PASSES):
+        picked_words, picked_scales = {}, {}
+
+        def pick(s):
             planes = tile([P, PACK, S], F32, f"planes{s}")
             for j in range(PACK):
-                window = x_raw[2 * s + j // 2][:, j % 2, :].indirect(offs_t[:])
-                if j < PACK - 1:
-                    nc.scalar.activation(planes[:, j, :], window, ACT.Copy)
-                else:
-                    nc.vector.tensor_copy(planes[:, j, :], window)
+                cut = X_NODES_ON_SCALAR[s][j]
+                if cut > 0:
+                    nc.scalar.activation(planes[:, j, :cut], x_planes[s][j].indirect(offs_t[:, : cut // 16]), ACT.Copy)
+                if cut < S:
+                    nc.vector.tensor_copy(planes[:, j, cut:], x_planes[s][j].indirect(offs_t[:, cut // 16 :]))
             grouped = tile([P, S * PACK], BF16, f"x_grouped{s}")
-            copy(False, *interleaved(grouped[:], planes[:]))
-            words = tile([P, S], U32, f"picked_words{s}")
-            scales = tile([P, S], U8, f"picked_scales{s}")
-            quantize(words, scales, grouped, slice(0, S))
-            picked_words.append(words)
-            picked_scales.append(scales)
+            dst, src = interleaved(grouped[:], planes[:])
+            cut = X_RUNS_ON_VECTOR[s]
+            copy(False, dst[:, :cut], src[:, :cut])
+            if cut < S // RUN:
+                copy(True, dst[:, cut:], src[:, cut:])
+            return grouped
+
+        def quantize_x(s, grouped, reuses=None):
+            picked_words[s] = tile([P, S], U32, f"picked_words{s}", reuses)
+            picked_scales[s] = tile([P, S], U8, f"picked_scales{s}")
+            quantize(picked_words[s], picked_scales[s], grouped, slice(0, S))
 
         def round_w1(g, s):
-            src = w1_raw[g][s][:].rearrange("p j (m u e) -> p u m j e", u=2, e=2)
+            src = w1_raw[g][s].rearrange("p j (m u e) -> p u m j e", u=2, e=2)
             pairs = []
             for u in range(2):
                 grouped = tile([P, 2 * P * PACK], BF16, f"w1_grouped{g}{s}{u}")
@@ -129,8 +147,8 @@ def tile_picked_sub_mlp_relu2_sub_e_kernel(tc, xT, w1, w2, gate, offs, pos1, pos
                             lhsT_scale=scales[:, e * P : (e + 1) * P],
                             rhs=picked_words[s][:, cols].bitcast(FP8X4),
                             rhs_scale=picked_scales[s][:, cols],
-                            start=(s == 0),
-                            stop=(s == PASSES - 1),
+                            start=(s == ORDER[0]),
+                            stop=(s == ORDER[-1]),
                         )
 
         def quantize_piece(g, s, pairs):
@@ -140,26 +158,10 @@ def tile_picked_sub_mlp_relu2_sub_e_kernel(tc, xT, w1, w2, gate, offs, pos1, pos
         halves = [slice(0, HALF), slice(HALF, S)]
 
         banks0 = [psum.tile([P, S], F32, name=f"bank0{t}", tag=f"b{t}") for t in range(PACK)]
-        for s in range(PASSES):
-            layer1_pass(s, quantize_piece(0, s, round_w1(0, s)), [banks0], [whole])
-        relu0 = tile([P, PACK, S], F32, "relu0")
-        nc.vector.tensor_scalar_max(relu0[:, 0, :], banks0[0][:], 0.0)
-        for t in (1, 2, 3):
-            nc.scalar.activation(relu0[:, t, :], banks0[t][:], ACT.Relu)
-        weights1 = [quantize_piece(1, 0, round_w1(1, 0))]
-        h0_grouped = tile([P, S * PACK], BF16, "h0_grouped")
-        for cols in halves:
-            nc.scalar.activation(*interleaved(h0_grouped[:, PACK * cols.start : PACK * cols.stop], relu0[:, :, cols]), ACT.Square)
-
         banks1 = [[psum.tile([P, 2, HALF], F32, name=f"bank1{h}{u}", tag=f"b{PACK + 2 * h + u}") for u in range(2)] for h in range(2)]
-        for s in range(PASSES):
-            if s > 0:
-                weights1.append(quantize_piece(1, s, round_w1(1, s)))
-            if s == 1:
-                h0_words = tile([P, HALF], U32, "h0_words", reuses="w1_grouped111")
-                h0_scales = tile([P, HALF], U8, "h0_scales")
-                quantize(h0_words, h0_scales, h0_grouped, halves[0])
-            for u, (words, scales) in weights1[s].items():
+
+        def group1_pass(s, weights):
+            for u, (words, scales) in weights.items():
                 for h, cols in enumerate(halves):
                     for e in range(2):
                         nc.tensor.matmul_mx(
@@ -168,21 +170,42 @@ def tile_picked_sub_mlp_relu2_sub_e_kernel(tc, xT, w1, w2, gate, offs, pos1, pos
                             lhsT_scale=scales[:, e * P : (e + 1) * P],
                             rhs=picked_words[s][:, cols].bitcast(FP8X4),
                             rhs_scale=picked_scales[s][:, cols],
-                            start=(s == 0 and e == 0),
-                            stop=(s == PASSES - 1 and e == 1),
+                            start=(s == ORDER[0] and e == 0),
+                            stop=(s == ORDER[-1] and e == 1),
                         )
 
-        late_words = tile([P, HALF], U32, "h0_late_words", reuses="w1_grouped121")
+        whole_weights = [quantize_piece(g, WHOLE, round_w1(g, WHOLE)) for g in range(GROUPS)]
+        quantize_x(0, pick(0))
+        quantize_x(1, pick(1))
+        layer1_pass(WHOLE, whole_weights[0], [banks0], [whole])
+        group1_pass(WHOLE, whole_weights[1])
+        quantize_x(2, pick(2))
+        for s in ORDER[1:]:
+            layer1_pass(s, quantize_piece(0, s, round_w1(0, s)), [banks0], [whole])
+        relu0 = tile([P, PACK, S], F32, "relu0")
+        for t in range(PACK):
+            nc.scalar.activation(relu0[:, t, :], banks0[t][:], ACT.Relu)
+        group1_pass(ORDER[1], quantize_piece(1, ORDER[1], round_w1(1, ORDER[1])))
+        h0_grouped = tile([P, S * PACK], BF16, "h0_grouped")
+
+        def square0(cols):
+            nc.scalar.activation(*interleaved(h0_grouped[:, PACK * cols.start : PACK * cols.stop], relu0[:, :, cols]), ACT.Square)
+
+        group1_pass(ORDER[2], quantize_piece(1, ORDER[2], round_w1(1, ORDER[2])))
+        for cols in halves:
+            square0(cols)
+        h0_words = tile([P, HALF], U32, "h0_words", reuses="w1_grouped121")
+        h0_scales = tile([P, HALF], U8, "h0_scales")
+        quantize(h0_words, h0_scales, h0_grouped, halves[0])
+        late_words = tile([P, HALF], U32, "h0_late_words", reuses="w1_words121")
         late_scales = tile([P, HALF], U8, "h0_late_scales")
         quantize(late_words, late_scales, h0_grouped[:, HALF * PACK :], halves[0])
 
         w2_grouped = tile([P, GROUPS * N * PACK], BF16, "w2_grouped")
-        w2_words = tile([P, GROUPS * N], U32, "w2_words", reuses="w1_words121")
+        w2_words = tile([P, GROUPS * N], U32, "w2_words", reuses="w1_words120")
         w2_scales = tile([P, GROUPS * N], U8, "w2_scales")
-        copy(True, *interleaved(w2_grouped[:, : N * PACK], w2_raw[0][:]))
-        dst, src = interleaved(w2_grouped[:, N * PACK :], w2_raw[1][:])
-        copy(True, dst[:, :W2_RUNS_ON_SCALAR], src[:, :W2_RUNS_ON_SCALAR])
-        copy(False, dst[:, W2_RUNS_ON_SCALAR:], src[:, W2_RUNS_ON_SCALAR:])
+        for g in range(GROUPS):
+            copy(False, *interleaved(w2_grouped[:, g * N * PACK : (g + 1) * N * PACK], w2_raw[g][:]))
 
         h1_grouped = tile([P, S * PACK], BF16, "h1_grouped")
         h1_words = tile([P, S], U32, "h1_words")

@@ -258,10 +258,9 @@ def tile_picked_sub_mlp_relu2_sub_e_kernel(tc, xT, w1, w2, gate, offs, pos1, pos
         nc.vector.tensor_tensor(terms[0][:], y[:].indirect(pos_t[0][:]), gate_t[:, 0, :], ALU.mult)
         nc.vector.tensor_tensor(terms[1][:, low], y[:].indirect(pos_t[1][:, : V // 32]), gate_t[:, 1, low], ALU.mult)
         nc.vector.tensor_tensor(terms[2][:], fetched[:], gate_t[:, 2, :], ALU.mult)
+        nc.vector.tensor_tensor(pair[:, low], terms[0][:, low], terms[1][:, low], ALU.add)
         nc.vector.tensor_tensor(terms[1][:, high], fetched_high[:], gate_t[:, 1, high], ALU.mult)
-        parts = [slice(0, V // 2), slice(V // 2, V)]
-        for part in parts:
-            nc.vector.tensor_tensor(pair[:, part], terms[0][:, part], terms[1][:, part], ALU.add)
-        for part, queue in zip(parts, (nc.sync, nc.scalar)):
-            nc.vector.tensor_tensor(result[:, part], pair[:, part], terms[2][:, part], ALU.add)
+        nc.vector.tensor_tensor(pair[:, high], terms[0][:, high], terms[2][:, high], ALU.add)
+        for part, last, queue in ((low, terms[2], nc.scalar), (high, terms[1], nc.sync)):
+            nc.vector.tensor_tensor(result[:, part], pair[:, part], last[:, part], ALU.add)
             queue.dma_start(out=out[:, part], in_=result[:, part])

@@ -261,6 +261,6 @@ def tile_picked_sub_mlp_relu2_sub_e_kernel(tc, xT, w1, w2, gate, offs, pos1, pos
         nc.vector.tensor_tensor(pair[:, low], terms[0][:, low], terms[1][:, low], ALU.add)
         nc.vector.tensor_tensor(terms[1][:, high], fetched_high[:], gate_t[:, 1, high], ALU.mult)
         nc.vector.tensor_tensor(pair[:, high], terms[0][:, high], terms[2][:, high], ALU.add)
-        for part, last, queue in ((low, terms[2], nc.scalar), (high, terms[1], nc.sync)):
+        for part, last, queue in ((low, terms[2], nc.sync), (high, terms[1], nc.scalar)):
             nc.vector.tensor_tensor(result[:, part], pair[:, part], last[:, part], ALU.add)
             queue.dma_start(out=out[:, part], in_=result[:, part])

@@ -261,6 +261,6 @@ def tile_picked_sub_mlp_relu2_sub_e_kernel(tc, xT, w1, w2, gate, offs, pos1, pos
         nc.vector.tensor_tensor(pair[:, low], terms[0][:, low], terms[1][:, low], ALU.add)
         nc.vector.tensor_tensor(terms[1][:, high], fetched_high[:], gate_t[:, 1, high], ALU.mult)
         nc.vector.tensor_tensor(pair[:, high], terms[0][:, high], terms[2][:, high], ALU.add)
-        for part, last, queue in ((low, terms[2], nc.sync), (high, terms[1], nc.scalar)):
+        for part, last in ((low, terms[2]), (high, terms[1])):
             nc.vector.tensor_tensor(result[:, part], pair[:, part], last[:, part], ALU.add)
-            queue.dma_start(out=out[:, part], in_=result[:, part])
+            nc.scalar.dma_start(out=out[:, part], in_=result[:, part])

@@ -174,12 +174,15 @@ def tile_picked_sub_mlp_relu2_sub_e_kernel(tc, xT, w1, w2, gate, offs, pos1, pos
                             stop=(s == ORDER[-1] and e == 1),
                         )
 
-        whole_weights = [quantize_piece(g, WHOLE, round_w1(g, WHOLE)) for g in range(GROUPS)]
+        whole_pairs = [round_w1(g, WHOLE) for g in range(GROUPS)]
+        whole_weights = [quantize_piece(0, WHOLE, whole_pairs[0]), {0: quantize_w1(1, WHOLE, 0, whole_pairs[1][0])}]
         quantize_x(0, pick(0))
         quantize_x(1, pick(1))
         layer1_pass(WHOLE, whole_weights[0], [banks0], [whole])
         group1_pass(WHOLE, whole_weights[1])
-        quantize_x(2, pick(2))
+        last_x = pick(2)
+        group1_pass(WHOLE, {1: quantize_w1(1, WHOLE, 1, whole_pairs[1][1], reuses="planes2")})
+        quantize_x(2, last_x)
         for s in ORDER[1:]:
             layer1_pass(s, quantize_piece(0, s, round_w1(0, s)), [banks0], [whole])
         relu0 = tile([P, PACK, S], F32, "relu0")

from contextlib import ExitStack

import concourse.mybir as mybir

K, T, S, H, N, D, V = 1536, 1024, 512, 1024, 128, 3, 256
FLOPS = 2 * S * (K * H + H * N)

F32 = mybir.dt.float32
BF16 = mybir.dt.bfloat16
U32 = mybir.dt.uint32
U16 = mybir.dt.uint16
U8 = mybir.dt.uint8
FP8X4 = mybir.dt.float8_e4m3fn_x4
ACT = mybir.ActivationFunctionType
ALU = mybir.AluOpType

P = 128
PACK = 4
K_PASS = P * PACK
PASSES = K // K_PASS
GROUPS = H // K_PASS
W = 512
RUN = 8
HALF = S // 2

X_RUNS_ON_VECTOR = (64, 64, 44)
X_NODES_ON_SCALAR = ((S, S, 0, 0), (S, S, S, 0), (S, 384, S, 0))
WHOLE = 1
ORDER = (1, 0, 2)
W1_ROWS_ON_VECTOR = (((0, 64), (P, 0), (64, 72)), ((P, P), (P, 64), (P, P)))
W2_RUNS_ON_SCALAR = 0
Y_BLOCKS = (slice(0, 256), slice(256, 384), slice(384, 512))


def tile_picked_sub_mlp_relu2_sub_e_kernel(tc, xT, w1, w2, gate, offs, pos1, pos2, pos3, out):
    nc = tc.nc
    with ExitStack() as ctx:
        keep = ctx.enter_context(tc.tile_pool(name="keep", bufs=1))
        psum = ctx.enter_context(tc.psum_pool(name="psum", bufs=1))

        def tile(shape, dtype, name, reuses=None):
            return keep.tile(shape, dtype, name=name, tag=reuses or name, align_bytes=64)

        def copy(on_scalar, dst, src):
            if on_scalar:
                nc.scalar.copy(dst, src)
            else:
                nc.vector.tensor_copy(out=dst, in_=src)

        def quantize(words, scales, grouped, cols, scale_row=0):
            nc.vector.quantize_mx(
                out=words[:, cols].bitcast(FP8X4),
                scales=scales[scale_row:P, cols],
                in_=grouped[:, PACK * cols.start : PACK * cols.stop],
            )

        def interleaved(grouped, planes):
            return (
                grouped.rearrange("p (c i j) -> p c j i", i=RUN, j=PACK),
                planes.rearrange("p j (c i) -> p c j i", i=RUN),
            )

        offs_t = keep.tile([P, S // 16], U16, name="offs_t")
        pos_t = [keep.tile([P, V // 16], U16, name=f"pos{d}_t") for d in range(D)]

        def load_rows(name, source, s, first, width):
            raw = tile([P, PACK, width], F32, name)
            rows = source[s * K_PASS : (s + 1) * K_PASS, first : first + width]
            nc.sync.dma_start(out=raw[:], in_=rows.rearrange("(p j) w -> p j w", j=PACK))
            return raw

        def load_x(s, half):
            raw = tile([P, 2, T], F32, f"x_raw{s}{half}")
            rows = xT[s * K_PASS : (s + 1) * K_PASS, :].rearrange("(p j) w -> p j w", j=PACK)
            nc.sync.dma_start(out=raw[:], in_=rows[:, 2 * half : 2 * half + 2, :])
            return raw

        w1_whole = load_rows("w1_whole", w1, WHOLE, 0, H)
        nc.sync.dma_start(offs_t[:], offs)
        x_whole = load_rows("x_raw0", xT, 0, 0, T)
        x_raw = [load_x(1 + n // 2, n % 2) for n in range(4)]
        x_planes = [
            [x_whole[:, j, :] for j in range(PACK)],
            [x_raw[j // 2][:, j % 2, :] for j in range(PACK)],
            [x_raw[2 + j // 2][:, j % 2, :] for j in range(PACK)],
        ]
        w1_raw = [
            {s: w1_whole[:, :, g * W : (g + 1) * W] if s == WHOLE else load_rows(f"w1_raw{g}{s}", w1, s, g * W, W)[:] for s in ORDER}
            for g in range(GROUPS)
        ]
        w2_raw = [load_rows(f"w2_raw{g}", w2, g, 0, N) for g in range(GROUPS)]
        gate_t = tile([P, D, V], F32, "gate_t")
        nc.sync.dma_start(out=gate_t[:], in_=gate.rearrange("d m v -> m d v"))
        for d, pos in enumerate((pos1, pos2, pos3)):
            nc.sync.dma_start(pos_t[d][:], pos)

        picked_words, picked_scales = {}, {}

        def pick(s):
            planes = tile([P, PACK, S], F32, f"planes{s}")
            for j in range(PACK):
                cut = X_NODES_ON_SCALAR[s][j]
                if cut > 0:
                    nc.scalar.activation(planes[:, j, :cut], x_planes[s][j].indirect(offs_t[:, : cut // 16]), ACT.Copy)
                if cut < S:
                    nc.vector.tensor_copy(planes[:, j, cut:], x_planes[s][j].indirect(offs_t[:, cut // 16 :]))
            grouped = tile([P, S * PACK], BF16, f"x_grouped{s}")
            dst, src = interleaved(grouped[:], planes[:])
            cut = X_RUNS_ON_VECTOR[s]
            copy(False, dst[:, :cut], src[:, :cut])
            if cut < S // RUN:
                copy(True, dst[:, cut:], src[:, cut:])
            return grouped

        def quantize_x(s, grouped, reuses=None):
            picked_words[s] = tile([P, S], U32, f"picked_words{s}", reuses)
            picked_scales[s] = tile([P, S], U8, f"picked_scales{s}")
            quantize(picked_words[s], picked_scales[s], grouped, slice(0, S))

        def round_w1(g, s):
            src = w1_raw[g][s].rearrange("p j (m u e) -> p u m j e", u=2, e=2)
            pairs = []
            for u in range(2):
                grouped = tile([P, 2 * P * PACK], BF16, f"w1_grouped{g}{s}{u}")
                dst = grouped[:].rearrange("p (e m j) -> p m j e", e=2, j=PACK)
                cut = W1_ROWS_ON_VECTOR[g][s][u]
                if cut > 0:
                    copy(False, dst[:, :cut], src[:, u, :cut])
                if cut < P:
                    copy(True, dst[:, cut:], src[:, u, cut:])
                pairs.append(grouped)
            return pairs

        def quantize_w1(g, s, u, grouped, reuses=None):
            words = tile([P, 2 * P], U32, f"w1_words{g}{s}{u}", reuses)
            scales = tile([P, 2 * P], U8, f"w1_scales{g}{s}{u}")
            quantize(words, scales, grouped, slice(0, 2 * P))
            return words, scales

        def layer1_pass(s, weights, banks, blocks):
            for block_banks, cols in zip(banks, blocks):
                for u, (words, scales) in weights.items():
                    for e in range(2):
                        nc.tensor.matmul_mx(
                            out=block_banks[2 * u + e][:],
                            lhsT=words[:, e * P : (e + 1) * P].bitcast(FP8X4),
                            lhsT_scale=scales[:, e * P : (e + 1) * P],
                            rhs=picked_words[s][:, cols].bitcast(FP8X4),
                            rhs_scale=picked_scales[s][:, cols],
                            start=(s == ORDER[0]),
                            stop=(s == ORDER[-1]),
                        )

        def quantize_piece(g, s, pairs):
            return {u: quantize_w1(g, s, u, pairs[u]) for u in range(2)}

        whole = slice(0, S)
        halves = [slice(0, HALF), slice(HALF, S)]

        banks0 = [psum.tile([P, S], F32, name=f"bank0{t}", tag=f"b{t}") for t in range(PACK)]
        banks1 = [[psum.tile([P, 2, HALF], F32, name=f"bank1{h}{u}", tag=f"b{PACK + 2 * h + u}") for u in range(2)] for h in range(2)]

        def group1_pass(s, weights):
            for u, (words, scales) in weights.items():
                for h, cols in enumerate(halves):
                    for e in range(2):
                        nc.tensor.matmul_mx(
                            out=banks1[h][u][:, e, :],
                            lhsT=words[:, e * P : (e + 1) * P].bitcast(FP8X4),
                            lhsT_scale=scales[:, e * P : (e + 1) * P],
                            rhs=picked_words[s][:, cols].bitcast(FP8X4),
                            rhs_scale=picked_scales[s][:, cols],
                            start=(s == ORDER[0] and e == 0),
                            stop=(s == ORDER[-1] and e == 1),
                        )

        whole_pairs = [round_w1(g, WHOLE) for g in range(GROUPS)]
        whole_weights = [quantize_piece(0, WHOLE, whole_pairs[0]), {0: quantize_w1(1, WHOLE, 0, whole_pairs[1][0])}]
        quantize_x(0, pick(0))
        quantize_x(1, pick(1))
        layer1_pass(WHOLE, whole_weights[0], [banks0], [whole])
        group1_pass(WHOLE, whole_weights[1])
        last_x = pick(2)
        group1_pass(WHOLE, {1: quantize_w1(1, WHOLE, 1, whole_pairs[1][1], reuses="planes2")})
        quantize_x(2, last_x)
        for s in ORDER[1:]:
            layer1_pass(s, quantize_piece(0, s, round_w1(0, s)), [banks0], [whole])
        relu0 = tile([P, PACK, S], F32, "relu0")
        for t in range(PACK):
            nc.scalar.activation(relu0[:, t, :], banks0[t][:], ACT.Relu)
        group1_pass(ORDER[1], quantize_piece(1, ORDER[1], round_w1(1, ORDER[1])))
        h0_grouped = tile([P, S * PACK], BF16, "h0_grouped")

        def square0(cols):
            nc.scalar.activation(*interleaved(h0_grouped[:, PACK * cols.start : PACK * cols.stop], relu0[:, :, cols]), ACT.Square)

        group1_pass(ORDER[2], quantize_piece(1, ORDER[2], round_w1(1, ORDER[2])))
        for cols in halves:
            square0(cols)
        h0_words = tile([P, HALF], U32, "h0_words", reuses="w1_grouped121")
        h0_scales = tile([P, HALF], U8, "h0_scales")
        quantize(h0_words, h0_scales, h0_grouped, halves[0])
        late_words = tile([P, HALF], U32, "h0_late_words", reuses="w1_words121")
        late_scales = tile([P, HALF], U8, "h0_late_scales")
        quantize(late_words, late_scales, h0_grouped[:, HALF * PACK :], halves[0])

        w2_grouped = tile([P, GROUPS * N * PACK], BF16, "w2_grouped")
        w2_words = tile([P, GROUPS * N], U32, "w2_words", reuses="w1_words120")
        w2_scales = tile([P, GROUPS * N], U8, "w2_scales")
        for g in range(GROUPS):
            copy(False, *interleaved(w2_grouped[:, g * N * PACK : (g + 1) * N * PACK], w2_raw[g][:]))

        h1_grouped = tile([P, S * PACK], BF16, "h1_grouped")
        h1_words = tile([P, S], U32, "h1_words")
        h1_scales = tile([P, S], U8, "h1_scales")
        both = tile([P, 2, S, 2], F32, "relu1")

        def woven(h, u, nodes):
            cols = slice(h * HALF + nodes.start, h * HALF + nodes.stop)
            return both[:, u, cols, :], banks1[h][u][:, :, nodes].rearrange("p e n -> p n e")

        nc.scalar.activation(*woven(0, 0, halves[0]), ACT.Relu)
        nc.vector.tensor_scalar_max(*woven(1, 0, halves[0]), 0.0)
        nc.scalar.activation(*woven(0, 1, halves[0]), ACT.Relu)
        nc.scalar.activation(*woven(1, 1, halves[0]), ACT.Relu)
        quantize(w2_words, w2_scales, w2_grouped, slice(0, GROUPS * N))
        for q in range(S // P):
            dst = h1_grouped[:, q * P * PACK : (q + 1) * P * PACK].rearrange("p (n u e) -> p n u e", u=2, e=2)
            src = both[:, :, q * P : (q + 1) * P, :].rearrange("p u n e -> p n u e")
            if q % 2 == 0:
                nc.scalar.activation(dst, src, ACT.Square)
            else:
                nc.vector.tensor_tensor(dst, src, src, ALU.mult)

        y = tile([P, S], F32, "y")
        for b, cols in enumerate(Y_BLOCKS):
            y_bank = psum.tile([P, cols.stop - cols.start], F32, name=f"y_bank{b}", tag=f"b{b}")
            quantize(h1_words, h1_scales, h1_grouped, cols)
            late = slice(cols.start - HALF, cols.stop - HALF)
            first = (h0_words[:, cols], h0_scales[:, cols]) if b == 0 else (late_words[:, late], late_scales[:, late])
            for g, (words, scales) in enumerate((first, (h1_words[:, cols], h1_scales[:, cols]))):
                nc.tensor.matmul_mx(
                    out=y_bank[:],
                    lhsT=w2_words[:, g * N : (g + 1) * N].bitcast(FP8X4),
                    lhsT_scale=w2_scales[:, g * N : (g + 1) * N],
                    rhs=words.bitcast(FP8X4),
                    rhs_scale=scales,
                    start=(g == 0),
                    stop=(g == GROUPS - 1),
                )
            copy(True, y[:, cols], y_bank[:])

        terms = [tile([P, V], F32, f"term{d}") for d in range(D)]
        pair = tile([P, V], F32, "pair")
        result = tile([P, V], F32, "result")
        low, high = slice(0, V // 2), slice(V // 2, V)
        fetched = tile([P, V], F32, "fetched")
        fetched_high = tile([P, V // 2], F32, "fetched_high")
        nc.scalar.activation(fetched[:], y[:].indirect(pos_t[2][:]), ACT.Copy)
        nc.scalar.activation(fetched_high[:], y[:].indirect(pos_t[1][:, V // 32 :]), ACT.Copy)
        nc.vector.tensor_tensor(terms[0][:], y[:].indirect(pos_t[0][:]), gate_t[:, 0, :], ALU.mult)
        nc.vector.tensor_tensor(terms[1][:, low], y[:].indirect(pos_t[1][:, : V // 32]), gate_t[:, 1, low], ALU.mult)
        nc.vector.tensor_tensor(terms[2][:], fetched[:], gate_t[:, 2, :], ALU.mult)
        nc.vector.tensor_tensor(pair[:, low], terms[0][:, low], terms[1][:, low], ALU.add)
        nc.vector.tensor_tensor(terms[1][:, high], fetched_high[:], gate_t[:, 1, high], ALU.mult)
        nc.vector.tensor_tensor(pair[:, high], terms[0][:, high], terms[2][:, high], ALU.add)
        for part, last in ((low, terms[2]), (high, terms[1])):
            nc.vector.tensor_tensor(result[:, part], pair[:, part], last[:, part], ALU.add)
            nc.scalar.dma_start(out=out[:, part], in_=result[:, part])
